import numpy as np, ml_dtypes
CORES = [100,101,102,103,108,109,110,111]
N = 8
R, L = 8192, 2048
CAPP = 512
def entries(a): return a.T.reshape(-1)
def pack(v, P): return np.ascontiguousarray(np.asarray(v, np.int32).reshape(-1, P).T)
def lists(rng, how):
    n = N * L
    P = rng.permutation(np.repeat(np.arange(N * N), CAPP))[:n]
    if how == "full":
        a, b = rng.permutation(N)[:2]; o = rng.permutation(N * N); o = o[(o // N != a) & (o % N != b)]
        C = np.concatenate([N * a + rng.permutation(np.delete(np.arange(N), b)), [N * a + b], N * rng.permutation(np.delete(np.arange(N), a)) + b, o])[:n // CAPP]
        P = np.repeat(C, CAPP).reshape(N, L)[rng.permutation(N)].reshape(-1)
    h, g = P // N, P % N
    d = np.zeros(n, np.int64)
    for q in range(N): m = np.nonzero(g == q)[0]; d[m] = R * q + np.concatenate([[0, R - 1], 1 + rng.permutation(R - 2)])[:len(m)]
    s = R * h + rng.integers(0, R, n)
    if how == "fork": s = R * h + rng.integers(0, R, N)[h]
    if how == "chain":
        for q in range(N):
            m = np.nonzero(h == q)[0]; w = d[g == q]
            if len(w): s[m] = w[rng.integers(0, len(w), len(m))]
    if how == "gaps":
        z = rng.permutation(N)[:3]; k = (rng.random(n) < 0.5) | (np.arange(n) // L == z[0]) | (h == z[1]) | (g == z[2]); s[k] = -1; d[k] = -1
    return {"src": np.stack([pack(v, 16) for v in s.reshape(N, L)]), "dst": np.stack([pack(v, 16) for v in d.reshape(N, L)])}
def setup_inputs(rng):
    return dict({"tab": rng.standard_normal((N, 128, R), dtype=np.float32).astype(ml_dtypes.bfloat16)}, **lists(rng, "uniform"))
def setup_inputs_chain(rng):
    d = setup_inputs(rng); d.update(lists(rng, "chain"))
    for k in ("tab",): d[k] = (d[k].astype(np.float32) * 1048576.0).astype(d[k].dtype)
    return d
def setup_inputs_fork(rng):
    d = setup_inputs(rng); d.update(lists(rng, "fork"))
    for k in ("tab",): d[k] = (d[k].astype(np.float32) * (1 / 1024.0)).astype(d[k].dtype)
    return d
def setup_inputs_full(rng):
    d = setup_inputs(rng); d.update(lists(rng, "full"))
    return d
def setup_inputs_gaps(rng):
    d = setup_inputs(rng); d.update(lists(rng, "gaps"))
    return d
def check_inputs(x):
    bad = []; s, d = x["src"].reshape(-1), x["dst"].reshape(-1); k = d >= 0
    if s.min() < -1 or s.max() >= N * R or d.min() < -1 or d.max() >= N * R: bad.append("out of range")
    if ((s < 0) != (d < 0)).any(): bad.append("half a pair")
    if len(np.unique(d[k])) != int(k.sum()): bad.append("a column is written twice")
    if k.any() and int(np.bincount(s[k] // R * N + d[k] // R).max()) > CAPP: bad.append("more than CAPP pairs from one rank's part to one rank's part")
    return bad
def reference(tab, src, dst):
    A = np.concatenate(list(tab), axis=1); Y = A.copy()
    for r in range(N):
        s, d = entries(src[r]), entries(dst[r]); k = d >= 0
        Y[:, d[k]] = A[:, s[k]]
    return {"y": np.stack([Y[:, R * r:R * r + R] for r in range(N)])}

@@ -1,0 +1,573 @@
+from concourse.bass import DstId, RemoteDMATransfer
+from concourse.mybir import AluOpType as A, ActivationFunctionType as F
+
+N, R, CAP = 8, 8192, 512
+SIM = 112
+MSG = 80
+B0 = 1025
+WW = B0 + N * CAP + 15
+CH = [512, 1024, 1024, 1024, 512]
+
+SCRATCH = {
+    "L": ("sbuf", [128, N * MSG], "bfloat16"),
+    "comb": ("sbuf", [128, R + N * CAP], "bfloat16"),
+    "G": ("sbuf", [128, N * CAP], "bfloat16"),
+    "YB": ("sbuf", [128, R], "bfloat16"),
+    "Wd": ("sbuf", [128, WW], "bfloat16"),
+    "IW": ("sbuf", [128, CAP + R], "bfloat16"),
+    "Z": ("sbuf", [128, 1024], "bfloat16"),
+    "PI": ("sbuf", [128, 8], "int32"),
+    "PF": ("sbuf", [128, 32], "float32"),
+    "DK": ("sbuf", [128, 128], "float32"),
+    "J128": ("sbuf", [128, 128], "float32"),
+    "Cc": ("sbuf", [128, 512], "float32"),
+    "Id": ("sbuf", [128, 128], "bfloat16"),
+    "Tri": ("sbuf", [128, 128], "bfloat16"),
+    "One": ("sbuf", [128, 128], "bfloat16"),
+    "M2": ("sbuf", [128, 8], "bfloat16"),
+    "Ex": ("sbuf", [128, 512], "bfloat16"),
+    "Wt": ("sbuf", [128, 1024], "bfloat16"),
+    "Rs": ("sbuf", [128, 512], "bfloat16"),
+    "BS": ("sbuf", [128, 144], "bfloat16"),
+    "BD": ("sbuf", [128, 144], "bfloat16"),
+    "SV": ("sbuf", [128, 512], "bfloat16"),
+    "NT": ("sbuf", [128, 32], "int32"),
+    "NU": ("sbuf", [128, 32], "int32"),
+    "KF": ("sbuf", [128, 16], "float32"),
+    "KI": ("sbuf", [128, 32], "bfloat16"),
+    "KZ": ("sbuf", [128, 32], "bfloat16"),
+    "XC": ("sbuf", [128, 64], "int32"),
+    "XL": ("sbuf", [128, 64], "int32"),
+    "XH": ("sbuf", [128, 64], "int32"),
+    "XF": ("sbuf", [128, 128], "float32"),
+    "U0": ("sbuf", [128, 1024], "bfloat16"),
+    "U1": ("sbuf", [128, 1024], "bfloat16"),
+    "M": ("sbuf", [128, 512], "bfloat16"),
+    "MS": ("sbuf", [128, 512], "bfloat16"),
+    "AM": ("sbuf", [128, 512], "bfloat16"),
+    "S0": ("sbuf", [128, 512], "bfloat16"),
+    "S1": ("sbuf", [128, 512], "bfloat16"),
+    "OF0": ("sbuf", [128, 64], "float32"),
+    "OF1": ("sbuf", [128, 64], "float32"),
+    "OU0": ("sbuf", [128, 64], "uint16"),
+    "OU1": ("sbuf", [128, 64], "uint16"),
+    "SO": ("sbuf", [128, 256], "uint16"),
+    "DS": ("sbuf", [128, 256], "float32"),
+    "DL": ("sbuf", [128, 256], "float32"),
+    "DX": ("sbuf", [128, 256], "float32"),
+    "OT": ("sbuf", [128, 32], "uint16"),
+    "IF": ("sbuf", [128, 512], "float32"),
+    "IU": ("sbuf", [128, 512], "uint16"),
+}
+for _k in range(8):
+    SCRATCH["b%d" % _k] = ("psum", [128, 512], "float32")
+NSEM = 130
+SEMAPHORES = ["la1", "la2", "dl", "dat", "hl", "hp0", "hp1", "hd", "lls", "ls"] + ["s%d" % k for k in range(NSEM)]
+
+
+def ones_of(mask):
+    return bin(mask).count("1")
+
+
+def split(mask, k):
+    bits = [b for b in range(32) if (mask >> b) & 1]
+    n = len(bits) // k
+    return [sum(1 << b for b in bits[i * n:(i + 1) * n]) for i in range(k)]
+
+
+def layout(T, topo):
+    cores = T.cores
+    info = []
+    for r in range(N):
+        c = cores[r]
+        here = [x for x in range(N) if topo.chip(cores[x]) == topo.chip(c)]
+        away = [x for x in range(N) if x not in here]
+        info.append({"core": c, "here": here, "away": away, "i": here.index(r), "helper": None})
+    for r in range(N):
+        f = info[r]
+        far = [cores[x] for x in f["away"]]
+        if all(topo.may_write(f["core"], x) for x in far):
+            continue
+        used = [i["helper"] for i in info]
+        free = [h for h in range(SIM) if topo.chip(h) == topo.chip(f["core"]) and h not in cores
+                and h not in used and all(topo.may_write(h, x) for x in far)]
+        f["helper"] = free[0]
+    for f in info:
+        i, n = f["i"], len(f["here"])
+        f["order"] = [f["away"][(i + k) % n] for k in range(n)] + [f["here"][(i + k) % n] for k in range(1, n)] + [f["here"][i]]
+        far = cores[f["away"][0]]
+        nb = cores[f["here"][(i + 1) % n]]
+        on = topo.mask(f["core"], nb)
+        src = f["core"] if f["helper"] is None else f["helper"]
+        f["off"] = topo.mask(src, far)
+        f["on"] = (on & ~f["off"]) if f["helper"] is None else on
+        f["full"] = on
+    return info
+
+
+def rank_program(g, core, T, topo):
+    info = layout(T, topo)
+    rank = T.rank_of(core)
+    if rank is None:
+        for r in range(N):
+            if info[r]["helper"] == core:
+                helper_program(g, T, topo, info, r)
+        return
+    member_program(g, core, T, topo, info, rank)
+
+
+def dst_id(topo, c):
+    rid, pid, _e = topo.addr(c)
+    return DstId(rid=rid, pnc=pid)
+
+
+def far_pair(g, T, topo, info, r, k, lsem):
+    f = info[r]
+    ms = split(f["off"], 2)
+    tr = []
+    for j in range(2):
+        d = info[f["order"][k + j]]["core"]
+        tr.append(RemoteDMATransfer(src=T.G[:, CAP * (k + j):CAP * (k + j + 1)], dst=T.comb[:, R + CAP * r:R + CAP * (r + 1)],
+                                    dst_ids=[dst_id(topo, d)], dma_engine_mask=ms[j], remote_sem=T.sem.dat))
+    g.remote_dma_fused(tr, local_sem=lsem)
+    return ones_of(f["off"])
+
+
+def far_targets(g, T, topo, info, r, lsem):
+    f = info[r]
+    ms = split(f["off"], 4)
+    tr = []
+    for k in range(4):
+        d = info[f["order"][k]]["core"]
+        tr.append(RemoteDMATransfer(src=T.DS[:, 32 * k:32 * k + 32], dst=T.DL[:, 32 * r:32 * r + 32],
+                                    dst_ids=[dst_id(topo, d)], dma_engine_mask=ms[k], remote_sem=T.sem.dl))
+    g.remote_dma_fused(tr, local_sem=lsem)
+    return ones_of(f["off"])
+
+
+def far_list(T, topo, info, r, slot):
+    f = info[r]
+    to = [info[x]["core"] for x in f["away"]]
+    z = 4 + f["i"]
+    return RemoteDMATransfer(src=T.L[:, MSG * slot:MSG * slot + MSG], dsts=[T.L[:, MSG * z:MSG * z + MSG] for _ in to],
+                             dst_ids=[dst_id(topo, c) for c in to], dma_engine_mask=f["off"], remote_sem=T.sem.la2)
+
+
+def helper_program(g, T, topo, info, r):
+    f = info[r]
+    tot = 0
+    g.wait_ge(T.sem.hl, ones_of(f["full"]))
+    g.remote_dma_fused([far_list(T, topo, info, r, f["i"])], local_sem=T.sem.ls)
+    tot += ones_of(f["off"])
+    g.wait_ge(T.sem.hp0, ones_of(f["full"]))
+    tot += far_pair(g, T, topo, info, r, 0, T.sem.ls)
+    g.wait_ge(T.sem.hd, ones_of(f["full"]))
+    tot += far_targets(g, T, topo, info, r, T.sem.ls)
+    g.wait_ge(T.sem.hp1, ones_of(f["full"]))
+    tot += far_pair(g, T, topo, info, r, 2, T.sem.ls)
+    g.wait_ge(T.sem.ls, tot)
+
+
+def member_program(g, core, T, topo, info, rank):
+    f = info[rank]
+    own = f["i"]
+    helper = f["helper"]
+    V, S, P, Y = g.vector, g.scalar, g.tensor, g.sync
+    queues = {"v": V, "s": S, "p": P, "y": Y, "g": g}
+    st = {"n": 0}
+    cur = {}
+    last = {}
+    seen = {}
+    waited = {}
+    allt = []
+
+    def new():
+        k = st["n"]
+        st["n"] = k + 1
+        return T.sem["s%d" % k], k
+
+    def op(q, inst):
+        if q not in cur:
+            sem, k = new()
+            cur[q] = [sem, k, 0]
+        c = cur[q]
+        inst.then_inc(c[0], 1)
+        c[2] += 1
+
+    def cut(q):
+        if q in cur:
+            c = cur.pop(q)
+            last[q] = (c[0], c[2], c[1])
+            allt.append(last[q])
+        return last[q]
+
+    def wait(q, *toks):
+        for t in toks:
+            if (q, t[2]) in seen:
+                continue
+            seen[(q, t[2])] = True
+            waited[t[2]] = True
+            queues[q].wait_ge(t[0], t[1])
+
+    def drain(q):
+        t = cut(q)
+        wait(q, t)
+        return t
+
+    def dmas(q, pairs):
+        sem, k = new()
+        for o, i in pairs:
+            queues[q].dma_start(o, i).then_inc(sem, 16)
+        t = (sem, 16 * len(pairs), k)
+        allt.append(t)
+        return t
+
+    t_nat = dmas("y", [(T.NT[:, 0:16], T.src[:]), (T.NT[:, 16:32], T.dst[:])])
+    t_xc = dmas("s", [(T.XC[0::4, :], T.src[:]), (T.XC[1::4, :], T.src[:]), (T.XC[2::4, :], T.dst[:]), (T.XC[3::4, :], T.dst[:])])
+    CUT = 2048
+    t_tab0 = dmas("y", [(T.comb[:, 0:CUT], T.tab[:, 0:CUT])])
+
+    op("g", g.iota(T.PI[:, 0:1], [[1, 1]], 0, 1))
+    t_i0 = cut("g")
+    op("g", g.iota(T.DK[:], [[1, 128]], 0, -1, allow_small_or_imprecise_dtypes=True))
+    t_i1 = cut("g")
+    op("g", g.iota(T.Cc[:], [[16, 512]], 0, 0, allow_small_or_imprecise_dtypes=True))
+    op("g", g.iota(T.J128[:], [[1, 128]], 0, 0, allow_small_or_imprecise_dtypes=True))
+    t_i2 = cut("g")
+
+    def vs(out, in0, s1, s2, o0, o1=None):
+        if o1 is None:
+            op("v", V.tensor_scalar(out, in0, s1, s2, o0))
+        else:
+            op("v", V.tensor_scalar(out, in0, s1, s2, o0, o1))
+
+    def vt(out, a, b, o):
+        op("v", V.tensor_tensor(out, a, b, o))
+
+    def pi(k):
+        return T.PI[:, k:k + 1]
+
+    def pf(k):
+        return T.PF[:, k:k + 1]
+
+    op("v", V.memset(T.Z[:], 0.0))
+    t_z = cut("v")
+    wait("v", t_i0)
+    vs(pi(1), pi(0), 15, None, A.bitwise_and)
+    vs(pi(2), pi(0), 4, None, A.logical_shift_right)
+    vs(pi(3), pi(0), 3, None, A.bitwise_and)
+    vs(pi(4), pi(0), 2, 3, A.logical_shift_right, A.bitwise_and)
+    vs(pi(5), pi(0), 4, 1, A.logical_shift_right, A.bitwise_and)
+    vs(pi(6), pi(0), 1, None, A.bitwise_and)
+    drain("v")
+    vs(pf(1), pi(5), 0, None, A.is_equal)
+    vs(pf(2), pi(5), 1, None, A.is_equal)
+    vs(pf(3), pi(6), 0, None, A.is_equal)
+    vs(pf(4), pi(6), 1, None, A.is_equal)
+    vs(pf(5), pi(3), 3, 4.0, A.is_equal, A.mult)
+    for s in range(4):
+        vs(pf(6 + s), pi(4), s, None, A.is_equal)
+    op("v", V.tensor_copy(pf(0), pi(1)))
+    vs(pf(10), pi(1), 0, None, A.is_equal)
+    vs(pf(11), pi(1), 1, None, A.is_equal)
+    vs(pf(12), pi(1), 1, 128.0, A.is_equal, A.mult)
+    vs(pf(13), pi(1), 2, None, A.is_equal)
+    vs(pf(19), pi(1), 3, 128.0, A.is_equal, A.mult)
+    vs(pf(18), pi(2), 4.0, 64.0, A.mult, A.add)
+    drain("v")
+    wait("v", t_i1)
+    vs(T.Id[:], T.DK[:], 0.0, None, A.is_equal)
+    for s in range(4):
+        vs(T.Ex[:, 128 * s:128 * s + 128], T.DK[:], -4.0 * s, pf(6 + s), A.is_equal, A.mult)
+
+    z = MSG * own
+    wait("v", t_nat)
+    vs(T.NU[:, 0:16], T.NT[:, 0:16], 10, 0xFFF8, A.arith_shift_right, A.bitwise_and)
+    vs(T.NU[:, 16:32], T.NT[:, 16:32], 13, None, A.arith_shift_right)
+    wait("v", t_xc)
+    vs(T.XL[:], T.XC[:], 127, None, A.bitwise_and)
+    vs(T.XH[:], T.XC[:], 7, 63, A.arith_shift_right, A.bitwise_and)
+    t_c0 = drain("v")
+    vt(T.KF[:], T.NU[:, 0:16], T.NU[:, 16:32], A.add)
+    vs(T.XF[:, 0:64], T.XL[:], pf(3), None, A.mult)
+    vs(T.XF[:, 64:128], T.XH[:], pf(4), pf(5), A.mult, A.add)
+    drain("v")
+    vs(T.KI[:, 0:16], T.KF[:], pf(1), None, A.mult)
+    vs(T.KI[:, 16:32], T.KF[:], pf(2), None, A.mult)
+    vt(T.L[:, z + 16:z + 80], T.XF[:, 0:64], T.XF[:, 64:128], A.add)
+    drain("v")
+    op("v", V.transpose(T.KZ[:], T.KI[:]))
+    drain("v")
+    vt(T.L[:, z:z + 16], T.KZ[:, 0:16], T.KZ[:, 16:32], A.add)
+    t_msg = cut("v")
+
+    wait("g", t_msg)
+    near = [info[x]["core"] for x in f["order"][4:7]]
+    zz = [T.L[:, z:z + MSG]]
+    if helper is None:
+        on = RemoteDMATransfer(src=T.L[:, z:z + MSG], dsts=zz * 3, dst_ids=[dst_id(topo, c) for c in near],
+                               dma_engine_mask=f["on"], remote_sem=T.sem.la1)
+        g.remote_dma_fused([far_list(T, topo, info, rank, own), on], local_sem=T.sem.lls)
+        nl = ones_of(f["on"]) + ones_of(f["off"])
+    else:
+        ms = split(f["full"], 2)
+        rid, pid, _e = topo.addr(helper)
+        g.remote_dma(T.L[:, z:z + MSG], T.L[:, z:z + MSG], T.sem.hl, T.sem.lls, pid, rid, f["full"])
+        on = RemoteDMATransfer(src=T.L[:, z:z + MSG], dsts=zz * 3, dst_ids=[dst_id(topo, c) for c in near],
+                               dma_engine_mask=f["on"], remote_sem=T.sem.la1)
+        g.remote_dma_fused([on], local_sem=T.sem.lls)
+        nl = ones_of(f["on"]) + ones_of(f["full"])
+    Y.wait_ge(T.sem.lls, nl)
+    t_tab1 = dmas("y", [(T.comb[:, CUT:R], T.tab[:, CUT:R])])
+
+    wait("s", t_z)
+    c0 = 0
+    while c0 < WW:
+        n = min(1024, WW - c0)
+        op("s", S.activation(T.Wd[:, c0:c0 + n], T.Z[:, 0:n], F.Copy))
+        c0 += n
+    t_wd = cut("s")
+
+    vs(T.Tri[:], T.DK[:], 0.0, None, A.is_gt)
+    op("v", V.memset(T.One[:], 1.0))
+    op("v", V.memset(T.M2[:], -2.0))
+    op("v", V.memset(T.Rs[:], 1.0))
+    for b in range(8):
+        vs(T.Wt[:, 128 * b:128 * b + 128], T.DK[:], 0.0, 256.0 * (5 + 2 * b), A.is_equal, A.mult)
+    drain("v")
+    op("v", V.memset(T.Rs[:, 0::64], 0.0))
+    wait("v", t_i2)
+    vs(T.Cc[:], T.Cc[:], pf(0), None, A.add)
+    t_const = drain("v")
+
+    banks = [(T.b0, T.b1, T.b2), (T.b5, T.b6, T.b7)]
+    t_u = None
+    t_sc = None
+    for pc in range(2):
+        bK, bA, bX = banks[pc]
+        Sb, OF, OU, U = (T.S0, T.OF0, T.OU0, T.U0) if pc == 0 else (T.S1, T.OF1, T.OU1, T.U1)
+        wait("p", t_c0, t_msg)
+        if pc == 0:
+            P.wait_ge(T.sem.la1, sum(ones_of(info[x]["on"]) for x in f["order"][4:7]))
+        else:
+            P.wait_ge(T.sem.la2, sum(ones_of(info[x]["off"]) for x in f["away"]))
+        for sl in range(4):
+            zl = MSG * (4 * pc + sl)
+            op("p", P.matmul(bK[:, 16 * sl:16 * sl + 16], T.Id[:], T.L[:, zl:zl + 16], True, True))
+        t_k = cut("p")
+        if pc == 1:
+            wait("p", t_u)
+        for sl in range(4):
+            zl = MSG * (4 * pc + sl)
+            bu = T.b3 if sl < 2 else T.b4
+            for s in range(4):
+                o = 256 * (sl % 2) + 64 * s
+                op("p", P.matmul(bu[:, o:o + 64], T.Ex[:, 128 * s:128 * s + 128], T.L[:, zl + 16:zl + 80], True, True))
+        t_up = cut("p")
+        wait("s", t_up)
+        op("s", S.activation(U[:, 0:512], T.b3[:], F.Copy))
+        op("s", S.activation(U[:, 512:1024], T.b4[:], F.Copy))
+        t_u = cut("s")
+        for blk in (range(0, 3) if pc == 0 else range(3, 8)):
+            op("s", S.activation(T.IW[:, CAP + 1024 * blk:CAP + 1024 * blk + 1024], T.Z[:], F.Copy))
+        t_iw = cut("s")
+        wait("v", t_k)
+        for b in range(8):
+            vs(T.M[:, 64 * b:64 * b + 64], bK[:, 0:64], float(8 * rank + f["order"][b]), None, A.is_equal)
+        t_m = drain("v")
+        op("v", V.tensor_tensor_scan(Sb[:], T.Rs[:], T.M[:], 0.0, A.mult, A.add))
+        t_s = drain("v")
+        vt(T.MS[:], T.M[:], Sb[:], A.mult)
+        t_ms = cut("v")
+        wait("p", t_const, t_m)
+        for b in range(8):
+            op("p", P.matmul(bX[:, 0:64], T.Wt[:, 128 * b:128 * b + 128], T.M[:, 64 * b:64 * b + 64], b == 0, False))
+        wait("p", t_s)
+        cut("p")
+        op("p", P.matmul(bA[:, 0:8], T.One[:], T.M2[:], True, False))
+        if pc == 1:
+            op("p", P.matmul(bA[:, 0:8], T.One[:], T.S0[:, 63::64], False, False))
+        op("p", P.matmul(bA[:, 0:8], T.Tri[:], Sb[:, 63::64], False, True))
+        t_a = cut("p")
+        wait("p", t_ms)
+        for b in range(8):
+            op("p", P.matmul(bX[:, 0:64], T.Id[:], T.MS[:, 64 * b:64 * b + 64], False, False))
+        wait("v", t_a)
+        for b in range(8):
+            vs(T.AM[:, 64 * b:64 * b + 64], bK[:, 0:64], float(8 * rank + f["order"][b]), bA[:, b:b + 1], A.is_equal, A.mult)
+        t_am = cut("v")
+        wait("p", t_am)
+        for b in range(8):
+            op("p", P.matmul(bX[:, 0:64], T.Id[:], T.AM[:, 64 * b:64 * b + 64], False, b == 7))
+        t_x = cut("p")
+        wait("v", t_x)
+        vt(OF[:], bX[:, 0:64], T.Cc[:, 0:64], A.max)
+        drain("v")
+        op("v", V.tensor_copy(OU[:], OF[:]))
+        drain("v")
+        wait("v", t_u, t_wd)
+        op("v", V.tensor_copy(T.Wd[:].indirect(OU[:]), U[:]))
+        if pc == 0:
+            vt(pf(12), pf(12), pf(10), A.add)
+            vt(pf(13), pf(13), pf(19), A.add)
+            for m in range(4):
+                vs(pf(14 + m), pf(18), float(m), pf(11), A.add, A.mult)
+            op("v", V.memset(T.BS[:], 0.0))
+            op("v", V.memset(T.BD[:], 0.0))
+            drain("v")
+            vs(T.BS[:, 15:143:16], T.One[:, 0:8], pf(12), None, A.mult)
+            vs(T.BD[:, 16 * rank + 15:16 * rank + 16], T.One[:, 0:1], pf(13), None, A.mult)
+            for m in range(4):
+                vs(T.SV[:, 128 * m:128 * m + 128], T.J128[:], pf(10), pf(14 + m), A.mult, A.add)
+            t_const2 = drain("v")
+        else:
+            t_sc = cut("v")
+
+    wait("p", t_const2, t_sc)
+
+    def rewrap(bank, W, c0, c1, lhs):
+        n = (c1 - c0) // 16
+        for q in range(16):
+            op("p", P.matmul(bank[:, 0:n], lhs[:, 15 - q:143 - q], W[:, c0 + q:c1:16], q == 0, q == 15))
+        return cut("p")
+
+    t_s0 = rewrap(T.b0, T.Wd, B0, B0 + 2048, T.BS)
+    t_d = rewrap(T.b2, T.Wd, B0, B0 + 4096, T.BD)
+    t_s1 = rewrap(T.b1, T.Wd, B0 + 2048, B0 + 4096, T.BS)
+
+    t_g = {}
+    wait("v", t_s0)
+    op("v", V.tensor_copy(T.SO[:, 0:128], T.b0[:, 0:128]))
+    t_so0 = drain("v")
+    wait("v", t_tab0, t_tab1)
+    wait("s", t_so0, t_tab0, t_tab1)
+    win = T.comb[:, 0:R]
+
+    def gath(q, k):
+        o = T.comb[:, R + CAP * rank:R + CAP * (rank + 1)] if k == 7 else T.G[:, CAP * k:CAP * (k + 1)]
+        i = win.indirect(T.SO[:, 32 * k:32 * k + 32])
+        if q == "v":
+            op(q, V.tensor_copy(o, i))
+        else:
+            op(q, S.activation(o, i, F.Copy))
+        t_g[k] = cut(q)
+
+    gath("v", 1)
+    gath("v", 3)
+    wait("v", t_s1)
+    op("v", V.tensor_copy(T.SO[:, 128:256], T.b1[:, 0:128]))
+    t_so1 = drain("v")
+    gath("s", 0)
+    gath("s", 2)
+    wait("s", t_d)
+    op("s", S.activation(T.DS[:], T.b2[:, 0:256], F.Copy))
+    op("s", S.activation(T.DL[:, 32 * rank:32 * rank + 32], T.b2[:, 224:256], F.Copy))
+    t_ds = cut("s")
+    wait("s", t_so1)
+    gath("s", 4)
+    gath("s", 6)
+    gath("v", 5)
+    gath("v", 7)
+
+    tot = 0
+    rid = pid = None
+    if helper is not None:
+        rid, pid, _e = topo.addr(helper)
+
+    def pair(k, hsem):
+        wait("g", t_g[k], t_g[k + 1])
+        if helper is None:
+            return far_pair(g, T, topo, info, rank, k, T.sem.ls)
+        g.remote_dma(T.G[:, CAP * k:CAP * (k + 2)], T.G[:, CAP * k:CAP * (k + 2)], hsem, T.sem.ls, pid, rid, f["full"])
+        return ones_of(f["full"])
+
+    tot += pair(0, T.sem.hp0)
+    wait("g", t_ds)
+    if helper is None:
+        tot += far_targets(g, T, topo, info, rank, T.sem.ls)
+    else:
+        g.remote_dma(T.DS[:, 0:128], T.DS[:, 0:128], T.sem.hd, T.sem.ls, pid, rid, f["full"])
+        tot += ones_of(f["full"])
+    tot += pair(2, T.sem.hp1)
+    ms = split(f["on"], 4)
+    tr = []
+    for k in range(4, 7):
+        tr.append(RemoteDMATransfer(src=T.DS[:, 32 * k:32 * k + 32], dst=T.DL[:, 32 * rank:32 * rank + 32],
+                                    dst_ids=[dst_id(topo, info[f["order"][k]]["core"])], dma_engine_mask=ms[k - 4], remote_sem=T.sem.dl))
+        tot += ones_of(ms[k - 4])
+    g.remote_dma_fused(tr, local_sem=T.sem.ls)
+    wait("g", t_g[4], t_g[5])
+    ms = split(f["on"], 2)
+    tr = []
+    for k in range(4, 6):
+        tr.append(RemoteDMATransfer(src=T.G[:, CAP * k:CAP * (k + 1)], dst=T.comb[:, R + CAP * rank:R + CAP * (rank + 1)],
+                                    dst_ids=[dst_id(topo, info[f["order"][k]]["core"])], dma_engine_mask=ms[k - 4], remote_sem=T.sem.dat))
+    g.remote_dma_fused(tr, local_sem=T.sem.ls)
+    tot += ones_of(f["on"])
+    wait("g", t_g[6])
+    rd, pd, _e = topo.addr(info[f["order"][6]]["core"])
+    g.remote_dma(T.comb[:, R + CAP * rank:R + CAP * (rank + 1)], T.G[:, CAP * 6:CAP * 7], T.sem.dat, T.sem.ls, pd, rd, f["on"])
+    tot += ones_of(f["on"])
+
+    ndl = ndat = 0
+    for x in range(N):
+        if x == rank:
+            continue
+        h = info[x]
+        k = h["order"].index(rank)
+        if k < 4:
+            ndl += ones_of(h["off"]) // 4
+            ndat += ones_of(h["off"]) // 2
+        else:
+            ndl += ones_of(h["on"]) // 4
+            ndat += ones_of(h["on"]) // (2 if k < 6 else 1)
+    V.wait_ge(T.sem.dl, ndl)
+    wait("v", t_ds)
+    vt(T.DX[:, 0:128], T.DL[:, 0:128], T.DL[:, 128:256], A.max)
+    drain("v")
+    vt(T.DX[:, 128:192], T.DX[:, 0:64], T.DX[:, 64:128], A.max)
+    drain("v")
+    vt(T.DX[:, 192:224], T.DX[:, 128:160], T.DX[:, 160:192], A.max)
+    drain("v")
+    vt(T.DX[:, 224:256], T.DX[:, 192:224], T.Cc[:, 0:32], A.max)
+    drain("v")
+    op("v", V.tensor_copy(T.OT[:], T.DX[:, 224:256]))
+    drain("v")
+    wait("v", t_iw)
+    op("v", V.tensor_copy(T.IW[:].indirect(T.OT[:]), T.SV[:]))
+    t_is = cut("v")
+    wait("p", t_is)
+    t_iu = []
+    t_ip = []
+    for h in range(2):
+        t_ip.append(rewrap(T.b3 if h == 0 else T.b4, T.IW, CAP + 4096 * h, CAP + 4096 * (h + 1), T.BS))
+    for h in range(2):
+        wait("v", t_ip[h])
+        vt(T.IF[:, 256 * h:256 * h + 256], (T.b3 if h == 0 else T.b4)[:, 0:256], T.Cc[:, 256 * h:256 * h + 256], A.max)
+        drain("v")
+        op("v", V.tensor_copy(T.IU[:, 256 * h:256 * h + 256], T.IF[:, 256 * h:256 * h + 256]))
+        t_iu.append(drain("v"))
+
+    V.wait_ge(T.sem.dat, ndat)
+    wait("v", t_g[7])
+    S.wait_ge(T.sem.dat, ndat)
+    wait("s", t_g[7], t_iu[1])
+    wins = T.comb[:]
+    cs = 0
+    stores = []
+    for n in CH:
+        for q in ("v", "s"):
+            a = cs if q == "v" else cs + 4096
+            i = wins.indirect(T.IU[:, a // 16:(a + n) // 16])
+            if q == "v":
+                op(q, V.tensor_copy(T.YB[:, a:a + n], i))
+            else:
+                op(q, S.activation(T.YB[:, a:a + n], i, F.Copy))
+            t = cut(q)
+            wait("y", t)
+            stores.append(dmas("y", [(T.y[:, a:a + n], T.YB[:, a:a + n])]))
+        cs += n
+    g.wait_ge(T.sem.ls, tot)
+    for t in allt:
+        if t[2] not in waited:
+            wait("g", t)

@@ -6,62 +6,24 @@ SIM = 112
 MSG = 80
 B0 = 1025
 WW = B0 + N * CAP + 15
-CH = [512, 1024, 1024, 1024, 512]
+CH = [256, 512, 768, 1024, 768, 512, 256]
 
-SCRATCH = {
-    "L": ("sbuf", [128, N * MSG], "bfloat16"),
-    "comb": ("sbuf", [128, R + N * CAP], "bfloat16"),
-    "G": ("sbuf", [128, N * CAP], "bfloat16"),
-    "YB": ("sbuf", [128, R], "bfloat16"),
-    "Wd": ("sbuf", [128, WW], "bfloat16"),
-    "IW": ("sbuf", [128, CAP + R], "bfloat16"),
-    "Z": ("sbuf", [128, 1024], "bfloat16"),
-    "PI": ("sbuf", [128, 8], "int32"),
-    "PF": ("sbuf", [128, 32], "float32"),
-    "DK": ("sbuf", [128, 128], "float32"),
-    "J128": ("sbuf", [128, 128], "float32"),
-    "Cc": ("sbuf", [128, 512], "float32"),
-    "Id": ("sbuf", [128, 128], "bfloat16"),
-    "Tri": ("sbuf", [128, 128], "bfloat16"),
-    "One": ("sbuf", [128, 128], "bfloat16"),
-    "M2": ("sbuf", [128, 8], "bfloat16"),
-    "Ex": ("sbuf", [128, 512], "bfloat16"),
-    "Wt": ("sbuf", [128, 1024], "bfloat16"),
-    "Rs": ("sbuf", [128, 512], "bfloat16"),
-    "BS": ("sbuf", [128, 144], "bfloat16"),
-    "BD": ("sbuf", [128, 144], "bfloat16"),
-    "SV": ("sbuf", [128, 512], "bfloat16"),
-    "NT": ("sbuf", [128, 32], "int32"),
-    "NU": ("sbuf", [128, 32], "int32"),
-    "KF": ("sbuf", [128, 16], "float32"),
-    "KI": ("sbuf", [128, 32], "bfloat16"),
-    "KZ": ("sbuf", [128, 32], "bfloat16"),
-    "XC": ("sbuf", [128, 64], "int32"),
-    "XL": ("sbuf", [128, 64], "int32"),
-    "XH": ("sbuf", [128, 64], "int32"),
-    "XF": ("sbuf", [128, 128], "float32"),
-    "U0": ("sbuf", [128, 1024], "bfloat16"),
-    "U1": ("sbuf", [128, 1024], "bfloat16"),
-    "M": ("sbuf", [128, 512], "bfloat16"),
-    "MS": ("sbuf", [128, 512], "bfloat16"),
-    "AM": ("sbuf", [128, 512], "bfloat16"),
-    "S0": ("sbuf", [128, 512], "bfloat16"),
-    "S1": ("sbuf", [128, 512], "bfloat16"),
-    "OF0": ("sbuf", [128, 64], "float32"),
-    "OF1": ("sbuf", [128, 64], "float32"),
-    "OU0": ("sbuf", [128, 64], "uint16"),
-    "OU1": ("sbuf", [128, 64], "uint16"),
-    "SO": ("sbuf", [128, 256], "uint16"),
-    "DS": ("sbuf", [128, 256], "float32"),
-    "DL": ("sbuf", [128, 256], "float32"),
-    "DX": ("sbuf", [128, 256], "float32"),
-    "OT": ("sbuf", [128, 32], "uint16"),
-    "IF": ("sbuf", [128, 512], "float32"),
-    "IU": ("sbuf", [128, 512], "uint16"),
-}
+SCRATCH = {"L": ("sbuf", [128, N * MSG], "bfloat16")}
+for _n, _w in (("comb", R + N * CAP), ("G", N * CAP), ("YB", R), ("Wd", WW), ("IW", CAP + R), ("Z", 512), ("Id", 128), ("Ih", 128),
+               ("Tri", 128), ("One", 128), ("M2", 8), ("Ex", 512), ("Wt", 1024), ("Rs", 512), ("E1", 32), ("SV", 512), ("KI", 32),
+               ("KZ", 32), ("U0", 1024), ("U1", 1024), ("M", 512), ("MS", 512), ("AM", 512), ("S0", 512), ("S1", 512), ("TB", 1024),
+               ("TI", 1024)):
+    SCRATCH[_n] = ("sbuf", [128, _w], "bfloat16")
+for _n, _w in (("PF", 32), ("DK", 128), ("J128", 128), ("Cc", 512), ("KF", 16), ("XF", 128), ("OF0", 64), ("OF1", 64), ("DS", 256),
+               ("DL", 256), ("DX", 256), ("IF", 512)):
+    SCRATCH[_n] = ("sbuf", [128, _w], "float32")
+for _n, _w in (("PI", 8), ("NT", 32), ("NU", 32), ("XC", 64), ("XL", 64), ("XH", 64)):
+    SCRATCH[_n] = ("sbuf", [128, _w], "int32")
+for _n, _w in (("OU0", 64), ("OU1", 64), ("SO", 256), ("OT", 32), ("IU", 512)):
+    SCRATCH[_n] = ("sbuf", [128, _w], "uint16")
 for _k in range(8):
     SCRATCH["b%d" % _k] = ("psum", [128, 512], "float32")
-NSEM = 130
+NSEM = 138
 SEMAPHORES = ["la1", "la2", "dl", "dat", "hl", "hp0", "hp1", "hd", "lls", "ls"] + ["s%d" % k for k in range(NSEM)]
 
 
@@ -133,16 +95,16 @@ def far_pair(g, T, topo, info, r, k, lsem):
     return ones_of(f["off"])
 
 
-def far_targets(g, T, topo, info, r, lsem):
+def targets(g, T, topo, info, r, ks, mask, lsem):
     f = info[r]
-    ms = split(f["off"], 4)
+    ms = split(mask, 4)
     tr = []
-    for k in range(4):
+    for j, k in enumerate(ks):
         d = info[f["order"][k]]["core"]
         tr.append(RemoteDMATransfer(src=T.DS[:, 32 * k:32 * k + 32], dst=T.DL[:, 32 * r:32 * r + 32],
-                                    dst_ids=[dst_id(topo, d)], dma_engine_mask=ms[k], remote_sem=T.sem.dl))
+                                    dst_ids=[dst_id(topo, d)], dma_engine_mask=ms[j], remote_sem=T.sem.dl))
     g.remote_dma_fused(tr, local_sem=lsem)
-    return ones_of(f["off"])
+    return ones_of(mask) // 4 * len(ks)
 
 
 def far_list(T, topo, info, r, slot):
@@ -155,14 +117,13 @@ def far_list(T, topo, info, r, slot):
 
 def helper_program(g, T, topo, info, r):
     f = info[r]
-    tot = 0
     g.wait_ge(T.sem.hl, ones_of(f["full"]))
     g.remote_dma_fused([far_list(T, topo, info, r, f["i"])], local_sem=T.sem.ls)
-    tot += ones_of(f["off"])
+    tot = ones_of(f["off"])
+    g.wait_ge(T.sem.hd, ones_of(f["full"]))
+    tot += targets(g, T, topo, info, r, range(4), f["off"], T.sem.ls)
     g.wait_ge(T.sem.hp0, ones_of(f["full"]))
     tot += far_pair(g, T, topo, info, r, 0, T.sem.ls)
-    g.wait_ge(T.sem.hd, ones_of(f["full"]))
-    tot += far_targets(g, T, topo, info, r, T.sem.ls)
     g.wait_ge(T.sem.hp1, ones_of(f["full"]))
     tot += far_pair(g, T, topo, info, r, 2, T.sem.ls)
     g.wait_ge(T.sem.ls, tot)
@@ -175,11 +136,7 @@ def member_program(g, core, T, topo, info, rank):
     V, S, P, Y = g.vector, g.scalar, g.tensor, g.sync
     queues = {"v": V, "s": S, "p": P, "y": Y, "g": g}
     st = {"n": 0}
-    cur = {}
-    last = {}
-    seen = {}
-    waited = {}
-    allt = []
+    cur, last, seen, waited, allt = {}, {}, {}, {}, []
 
     def new():
         k = st["n"]
@@ -222,19 +179,6 @@ def member_program(g, core, T, topo, info, rank):
         allt.append(t)
         return t
 
-    t_nat = dmas("y", [(T.NT[:, 0:16], T.src[:]), (T.NT[:, 16:32], T.dst[:])])
-    t_xc = dmas("s", [(T.XC[0::4, :], T.src[:]), (T.XC[1::4, :], T.src[:]), (T.XC[2::4, :], T.dst[:]), (T.XC[3::4, :], T.dst[:])])
-    CUT = 2048
-    t_tab0 = dmas("y", [(T.comb[:, 0:CUT], T.tab[:, 0:CUT])])
-
-    op("g", g.iota(T.PI[:, 0:1], [[1, 1]], 0, 1))
-    t_i0 = cut("g")
-    op("g", g.iota(T.DK[:], [[1, 128]], 0, -1, allow_small_or_imprecise_dtypes=True))
-    t_i1 = cut("g")
-    op("g", g.iota(T.Cc[:], [[16, 512]], 0, 0, allow_small_or_imprecise_dtypes=True))
-    op("g", g.iota(T.J128[:], [[1, 128]], 0, 0, allow_small_or_imprecise_dtypes=True))
-    t_i2 = cut("g")
-
     def vs(out, in0, s1, s2, o0, o1=None):
         if o1 is None:
             op("v", V.tensor_scalar(out, in0, s1, s2, o0))
@@ -244,41 +188,47 @@ def member_program(g, core, T, topo, info, rank):
     def vt(out, a, b, o):
         op("v", V.tensor_tensor(out, a, b, o))
 
+    def vc(out, a):
+        op("v", V.tensor_copy(out, a))
+
+    def sc(out, a):
+        op("s", S.activation(out, a, F.Copy))
+
+    def mm(out, l, r, a, b):
+        op("p", P.matmul(out, l, r, a, b))
+
     def pi(k):
         return T.PI[:, k:k + 1]
 
     def pf(k):
         return T.PF[:, k:k + 1]
 
-    op("v", V.memset(T.Z[:], 0.0))
-    t_z = cut("v")
+    t_nat = dmas("y", [(T.NT[:, 0:16], T.src[:]), (T.NT[:, 16:32], T.dst[:])])
+    t_xc = dmas("s", [(T.XC[0::4, :], T.src[:]), (T.XC[1::4, :], T.src[:]), (T.XC[2::4, :], T.dst[:]), (T.XC[3::4, :], T.dst[:])])
+
+    op("g", g.iota(T.PI[:, 0:1], [[1, 1]], 0, 1))
+    t_i0 = cut("g")
+    op("g", g.iota(T.DK[:], [[1, 128]], 0, -1, allow_small_or_imprecise_dtypes=True))
+    t_i1 = cut("g")
+    op("g", g.iota(T.Cc[:], [[16, 512]], 0, 0, allow_small_or_imprecise_dtypes=True))
+    op("g", g.iota(T.J128[:], [[1, 128]], 0, 0, allow_small_or_imprecise_dtypes=True))
+    t_i2 = cut("g")
+
     wait("v", t_i0)
-    vs(pi(1), pi(0), 15, None, A.bitwise_and)
-    vs(pi(2), pi(0), 4, None, A.logical_shift_right)
-    vs(pi(3), pi(0), 3, None, A.bitwise_and)
-    vs(pi(4), pi(0), 2, 3, A.logical_shift_right, A.bitwise_and)
     vs(pi(5), pi(0), 4, 1, A.logical_shift_right, A.bitwise_and)
     vs(pi(6), pi(0), 1, None, A.bitwise_and)
+    vs(pi(3), pi(0), 3, None, A.bitwise_and)
+    vs(pi(1), pi(0), 15, None, A.bitwise_and)
+    vs(pi(2), pi(0), 4, None, A.logical_shift_right)
+    vs(pi(4), pi(0), 2, 3, A.logical_shift_right, A.bitwise_and)
     drain("v")
     vs(pf(1), pi(5), 0, None, A.is_equal)
     vs(pf(2), pi(5), 1, None, A.is_equal)
     vs(pf(3), pi(6), 0, None, A.is_equal)
     vs(pf(4), pi(6), 1, None, A.is_equal)
     vs(pf(5), pi(3), 3, 4.0, A.is_equal, A.mult)
-    for s in range(4):
-        vs(pf(6 + s), pi(4), s, None, A.is_equal)
-    op("v", V.tensor_copy(pf(0), pi(1)))
-    vs(pf(10), pi(1), 0, None, A.is_equal)
-    vs(pf(11), pi(1), 1, None, A.is_equal)
-    vs(pf(12), pi(1), 1, 128.0, A.is_equal, A.mult)
-    vs(pf(13), pi(1), 2, None, A.is_equal)
-    vs(pf(19), pi(1), 3, 128.0, A.is_equal, A.mult)
-    vs(pf(18), pi(2), 4.0, 64.0, A.mult, A.add)
-    drain("v")
-    wait("v", t_i1)
-    vs(T.Id[:], T.DK[:], 0.0, None, A.is_equal)
-    for s in range(4):
-        vs(T.Ex[:, 128 * s:128 * s + 128], T.DK[:], -4.0 * s, pf(6 + s), A.is_equal, A.mult)
+    op("v", V.memset(T.Z[:], 0.0))
+    t_z = cut("v")
 
     z = MSG * own
     wait("v", t_nat)
@@ -287,7 +237,8 @@ def member_program(g, core, T, topo, info, rank):
     wait("v", t_xc)
     vs(T.XL[:], T.XC[:], 127, None, A.bitwise_and)
     vs(T.XH[:], T.XC[:], 7, 63, A.arith_shift_right, A.bitwise_and)
-    t_c0 = drain("v")
+    wait("v", t_z)
+    drain("v")
     vt(T.KF[:], T.NU[:, 0:16], T.NU[:, 16:32], A.add)
     vs(T.XF[:, 0:64], T.XL[:], pf(3), None, A.mult)
     vs(T.XF[:, 64:128], T.XH[:], pf(4), pf(5), A.mult, A.add)
@@ -303,57 +254,80 @@ def member_program(g, core, T, topo, info, rank):
 
     wait("g", t_msg)
     near = [info[x]["core"] for x in f["order"][4:7]]
-    zz = [T.L[:, z:z + MSG]]
+    mine = T.L[:, z:z + MSG]
+    on = RemoteDMATransfer(src=mine, dsts=[mine] * 3, dst_ids=[dst_id(topo, c) for c in near],
+                           dma_engine_mask=f["on"], remote_sem=T.sem.la1)
+    rid = pid = None
     if helper is None:
-        on = RemoteDMATransfer(src=T.L[:, z:z + MSG], dsts=zz * 3, dst_ids=[dst_id(topo, c) for c in near],
-                               dma_engine_mask=f["on"], remote_sem=T.sem.la1)
         g.remote_dma_fused([far_list(T, topo, info, rank, own), on], local_sem=T.sem.lls)
         nl = ones_of(f["on"]) + ones_of(f["off"])
     else:
-        ms = split(f["full"], 2)
         rid, pid, _e = topo.addr(helper)
-        g.remote_dma(T.L[:, z:z + MSG], T.L[:, z:z + MSG], T.sem.hl, T.sem.lls, pid, rid, f["full"])
-        on = RemoteDMATransfer(src=T.L[:, z:z + MSG], dsts=zz * 3, dst_ids=[dst_id(topo, c) for c in near],
-                               dma_engine_mask=f["on"], remote_sem=T.sem.la1)
         g.remote_dma_fused([on], local_sem=T.sem.lls)
+        g.remote_dma(mine, mine, T.sem.hl, T.sem.lls, pid, rid, f["full"])
         nl = ones_of(f["on"]) + ones_of(f["full"])
     Y.wait_ge(T.sem.lls, nl)
-    t_tab1 = dmas("y", [(T.comb[:, CUT:R], T.tab[:, CUT:R])])
+    t_tab = dmas("y", [(T.comb[:, 0:R], T.tab[:])])
+
+    wait("v", t_i1)
+    vs(T.Id[:], T.DK[:], 0.0, None, A.is_equal)
+    for s in range(4):
+        vs(pf(6 + s), pi(4), s, None, A.is_equal)
+    vc(pf(0), pi(1))
+    vs(pf(10), pi(1), 0, None, A.is_equal)
+    vs(pf(11), pi(1), 1, None, A.is_equal)
+    vs(pf(12), pi(1), 2, None, A.is_equal)
+    vs(pf(13), pi(1), 3, None, A.is_equal)
+    vs(pf(18), pi(2), 4.0, 64.0, A.mult, A.add)
+    op("v", V.memset(T.One[:], 1.0))
+    op("v", V.memset(T.M2[:], -2.0))
+    op("v", V.memset(T.Rs[:], 1.0))
+    op("v", V.memset(T.E1[:, 16:32], 0.0))
+    drain("v")
+    for s in range(4):
+        vs(T.Ex[:, 128 * s:128 * s + 128], T.DK[:], -4.0 * s, pf(6 + s), A.is_equal, A.mult)
+    for m in range(4):
+        vs(pf(14 + m), pf(18), float(m), pf(11), A.add, A.mult)
+    t_pf = cut("v")
+    vs(T.Tri[:], T.DK[:], 0.0, None, A.is_gt)
+    for b in range(8):
+        vs(T.Wt[:, 128 * b:128 * b + 128], T.DK[:], 0.0, 256.0 * (5 + 2 * b), A.is_equal, A.mult)
+    vs(T.Ih[:], T.DK[:], 0.0, 128.0, A.is_equal, A.mult)
+    op("v", V.memset(T.Rs[:, 0::64], 0.0))
+    wait("v", t_i2)
+    vs(T.Cc[:, 0:64], T.Cc[:, 0:64], pf(0), None, A.add)
+    vs(T.E1[:, 0:8], T.One[:, 0:8], pf(10), None, A.mult)
+    vs(T.E1[:, 8:16], T.One[:, 0:8], pf(11), None, A.mult)
+    vc(T.E1[:, 16 + rank:17 + rank], pf(12))
+    vc(T.E1[:, 24 + rank:25 + rank], pf(13))
+    t_const = drain("v")
 
     wait("s", t_z)
     c0 = 0
     while c0 < WW:
-        n = min(1024, WW - c0)
-        op("s", S.activation(T.Wd[:, c0:c0 + n], T.Z[:, 0:n], F.Copy))
+        n = min(512, WW - c0)
+        sc(T.Wd[:, c0:c0 + n], T.Z[:, 0:n])
         c0 += n
     t_wd = cut("s")
-
-    vs(T.Tri[:], T.DK[:], 0.0, None, A.is_gt)
-    op("v", V.memset(T.One[:], 1.0))
-    op("v", V.memset(T.M2[:], -2.0))
-    op("v", V.memset(T.Rs[:], 1.0))
-    for b in range(8):
-        vs(T.Wt[:, 128 * b:128 * b + 128], T.DK[:], 0.0, 256.0 * (5 + 2 * b), A.is_equal, A.mult)
-    drain("v")
-    op("v", V.memset(T.Rs[:, 0::64], 0.0))
-    wait("v", t_i2)
-    vs(T.Cc[:], T.Cc[:], pf(0), None, A.add)
-    t_const = drain("v")
+    wait("s", t_pf, t_i2)
+    op("s", S.activation(T.Cc[:, 64:512], T.Cc[:, 64:512], F.Identity, bias=pf(0)))
+    for m in range(4):
+        op("s", S.activation(T.SV[:, 128 * m:128 * m + 128], T.J128[:], F.Identity, bias=pf(14 + m), scale=pf(10)))
+    t_sv = cut("s")
 
     banks = [(T.b0, T.b1, T.b2), (T.b5, T.b6, T.b7)]
     t_u = None
-    t_sc = None
     for pc in range(2):
         bK, bA, bX = banks[pc]
         Sb, OF, OU, U = (T.S0, T.OF0, T.OU0, T.U0) if pc == 0 else (T.S1, T.OF1, T.OU1, T.U1)
-        wait("p", t_c0, t_msg)
+        wait("p", t_msg, t_pf)
         if pc == 0:
             P.wait_ge(T.sem.la1, sum(ones_of(info[x]["on"]) for x in f["order"][4:7]))
         else:
             P.wait_ge(T.sem.la2, sum(ones_of(info[x]["off"]) for x in f["away"]))
         for sl in range(4):
             zl = MSG * (4 * pc + sl)
-            op("p", P.matmul(bK[:, 16 * sl:16 * sl + 16], T.Id[:], T.L[:, zl:zl + 16], True, True))
+            mm(bK[:, 16 * sl:16 * sl + 16], T.Id[:], T.L[:, zl:zl + 16], True, True)
         t_k = cut("p")
         if pc == 1:
             wait("p", t_u)
@@ -362,14 +336,14 @@ def member_program(g, core, T, topo, info, rank):
             bu = T.b3 if sl < 2 else T.b4
             for s in range(4):
                 o = 256 * (sl % 2) + 64 * s
-                op("p", P.matmul(bu[:, o:o + 64], T.Ex[:, 128 * s:128 * s + 128], T.L[:, zl + 16:zl + 80], True, True))
+                mm(bu[:, o:o + 64], T.Ex[:, 128 * s:128 * s + 128], T.L[:, zl + 16:zl + 80], True, True)
         t_up = cut("p")
         wait("s", t_up)
-        op("s", S.activation(U[:, 0:512], T.b3[:], F.Copy))
-        op("s", S.activation(U[:, 512:1024], T.b4[:], F.Copy))
+        sc(U[:, 0:512], T.b3[:])
+        sc(U[:, 512:1024], T.b4[:])
         t_u = cut("s")
-        for blk in (range(0, 3) if pc == 0 else range(3, 8)):
-            op("s", S.activation(T.IW[:, CAP + 1024 * blk:CAP + 1024 * blk + 1024], T.Z[:], F.Copy))
+        for blk in (range(0, 6) if pc == 0 else range(6, 16)):
+            sc(T.IW[:, CAP + 512 * blk:CAP + 512 * blk + 512], T.Z[:])
         t_iw = cut("s")
         wait("v", t_k)
         for b in range(8):
@@ -381,88 +355,98 @@ def member_program(g, core, T, topo, info, rank):
         t_ms = cut("v")
         wait("p", t_const, t_m)
         for b in range(8):
-            op("p", P.matmul(bX[:, 0:64], T.Wt[:, 128 * b:128 * b + 128], T.M[:, 64 * b:64 * b + 64], b == 0, False))
+            mm(bX[:, 0:64], T.Wt[:, 128 * b:128 * b + 128], T.M[:, 64 * b:64 * b + 64], b == 0, False)
         wait("p", t_s)
         cut("p")
-        op("p", P.matmul(bA[:, 0:8], T.One[:], T.M2[:], True, False))
+        mm(bA[:, 0:8], T.One[:], T.M2[:], True, False)
         if pc == 1:
-            op("p", P.matmul(bA[:, 0:8], T.One[:], T.S0[:, 63::64], False, False))
-        op("p", P.matmul(bA[:, 0:8], T.Tri[:], Sb[:, 63::64], False, True))
+            mm(bA[:, 0:8], T.One[:], T.S0[:, 63::64], False, False)
+        mm(bA[:, 0:8], T.Tri[:], Sb[:, 63::64], False, True)
         t_a = cut("p")
         wait("p", t_ms)
         for b in range(8):
-            op("p", P.matmul(bX[:, 0:64], T.Id[:], T.MS[:, 64 * b:64 * b + 64], False, False))
+            mm(bX[:, 0:64], T.Id[:], T.MS[:, 64 * b:64 * b + 64], False, False)
         wait("v", t_a)
         for b in range(8):
             vs(T.AM[:, 64 * b:64 * b + 64], bK[:, 0:64], float(8 * rank + f["order"][b]), bA[:, b:b + 1], A.is_equal, A.mult)
         t_am = cut("v")
         wait("p", t_am)
         for b in range(8):
-            op("p", P.matmul(bX[:, 0:64], T.Id[:], T.AM[:, 64 * b:64 * b + 64], False, b == 7))
+            mm(bX[:, 0:64], T.Id[:], T.AM[:, 64 * b:64 * b + 64], False, b == 7)
         t_x = cut("p")
         wait("v", t_x)
         vt(OF[:], bX[:, 0:64], T.Cc[:, 0:64], A.max)
         drain("v")
-        op("v", V.tensor_copy(OU[:], OF[:]))
+        vc(OU[:], OF[:])
         drain("v")
         wait("v", t_u, t_wd)
-        op("v", V.tensor_copy(T.Wd[:].indirect(OU[:]), U[:]))
-        if pc == 0:
-            vt(pf(12), pf(12), pf(10), A.add)
-            vt(pf(13), pf(13), pf(19), A.add)
-            for m in range(4):
-                vs(pf(14 + m), pf(18), float(m), pf(11), A.add, A.mult)
-            op("v", V.memset(T.BS[:], 0.0))
-            op("v", V.memset(T.BD[:], 0.0))
-            drain("v")
-            vs(T.BS[:, 15:143:16], T.One[:, 0:8], pf(12), None, A.mult)
-            vs(T.BD[:, 16 * rank + 15:16 * rank + 16], T.One[:, 0:1], pf(13), None, A.mult)
-            for m in range(4):
-                vs(T.SV[:, 128 * m:128 * m + 128], T.J128[:], pf(10), pf(14 + m), A.mult, A.add)
-            t_const2 = drain("v")
-        else:
-            t_sc = cut("v")
+        vc(T.Wd[:].indirect(OU[:]), U[:])
+        t_sc = drain("v") if pc == 0 else cut("v")
 
-    wait("p", t_const2, t_sc)
-
-    def rewrap(bank, W, c0, c1, lhs):
-        n = (c1 - c0) // 16
+    def turn(bank, W, c0, n):
         for q in range(16):
-            op("p", P.matmul(bank[:, 0:n], lhs[:, 15 - q:143 - q], W[:, c0 + q:c1:16], q == 0, q == 15))
+            mm(bank[:, q:16 * n:16], W[:, c0 + q:c0 + 2048:16], T.E1[:, 0:n], True, True)
         return cut("p")
 
-    t_s0 = rewrap(T.b0, T.Wd, B0, B0 + 2048, T.BS)
-    t_d = rewrap(T.b2, T.Wd, B0, B0 + 4096, T.BD)
-    t_s1 = rewrap(T.b1, T.Wd, B0 + 2048, B0 + 4096, T.BS)
+    def back(bank, tb, c):
+        mm(bank[:, 0:128], tb[:, c:c + 128], T.Id[:], True, False)
+        mm(bank[:, 0:128], tb[:, c + 128:c + 256], T.Ih[:], False, True)
+        return cut("p")
 
     t_g = {}
-    wait("v", t_s0)
-    op("v", V.tensor_copy(T.SO[:, 0:128], T.b0[:, 0:128]))
-    t_so0 = drain("v")
-    wait("v", t_tab0, t_tab1)
-    wait("s", t_so0, t_tab0, t_tab1)
     win = T.comb[:, 0:R]
 
     def gath(q, k):
         o = T.comb[:, R + CAP * rank:R + CAP * (rank + 1)] if k == 7 else T.G[:, CAP * k:CAP * (k + 1)]
         i = win.indirect(T.SO[:, 32 * k:32 * k + 32])
         if q == "v":
-            op(q, V.tensor_copy(o, i))
+            vc(o, i)
         else:
-            op(q, S.activation(o, i, F.Copy))
+            sc(o, i)
         t_g[k] = cut(q)
 
+    wait("p", t_sc)
+    t_h0 = turn(T.b0, T.Wd, B0, 32)
+    wait("v", t_h0)
+    vc(T.TB[:, 0:256], T.b0[:, 0:256])
+    t_t0 = cut("v")
+    wait("p", t_t0)
+    t_s0 = back(T.b1, T.TB, 0)
+    wait("s", t_t0)
+    sc(T.TB[:, 256:512], T.b0[:, 256:512])
+    t_t1 = cut("s")
+    wait("p", t_t1)
+    t_d0 = back(T.b2, T.TB, 256)
+    t_h1 = turn(T.b5, T.Wd, B0 + 2048, 32)
+    wait("v", t_s0)
+    vc(T.SO[:, 0:128], T.b1[:, 0:128])
+    t_so0 = drain("v")
+    wait("v", t_tab)
     gath("v", 1)
+    wait("v", t_h1)
+    vc(T.TB[:, 512:768], T.b5[:, 0:256])
+    t_t2 = cut("v")
     gath("v", 3)
-    wait("v", t_s1)
-    op("v", V.tensor_copy(T.SO[:, 128:256], T.b1[:, 0:128]))
-    t_so1 = drain("v")
+    wait("p", t_t2)
+    t_s1 = back(T.b6, T.TB, 512)
+    wait("s", t_d0)
+    sc(T.DS[:, 0:128], T.b2[:, 0:128])
+    t_ds0 = cut("s")
+    wait("s", t_so0, t_tab)
     gath("s", 0)
     gath("s", 2)
-    wait("s", t_d)
-    op("s", S.activation(T.DS[:], T.b2[:, 0:256], F.Copy))
-    op("s", S.activation(T.DL[:, 32 * rank:32 * rank + 32], T.b2[:, 224:256], F.Copy))
-    t_ds = cut("s")
+    wait("s", t_t2)
+    sc(T.TB[:, 768:1024], T.b5[:, 256:512])
+    t_t3 = cut("s")
+    wait("p", t_t3)
+    t_d1 = back(T.b7, T.TB, 768)
+    wait("v", t_s1)
+    vc(T.SO[:, 128:256], T.b6[:, 0:128])
+    t_so1 = drain("v")
+    wait("s", t_d1)
+    sc(T.DS[:, 128:256], T.b7[:, 0:128])
+    sc(T.DL[:, 32 * rank:32 * rank + 32], T.b7[:, 96:128])
+    t_ds1 = cut("s")
     wait("s", t_so1)
     gath("s", 4)
     gath("s", 6)
@@ -470,43 +454,33 @@ def member_program(g, core, T, topo, info, rank):
     gath("v", 7)
 
     tot = 0
-    rid = pid = None
-    if helper is not None:
-        rid, pid, _e = topo.addr(helper)
-
-    def pair(k, hsem):
-        wait("g", t_g[k], t_g[k + 1])
-        if helper is None:
-            return far_pair(g, T, topo, info, rank, k, T.sem.ls)
-        g.remote_dma(T.G[:, CAP * k:CAP * (k + 2)], T.G[:, CAP * k:CAP * (k + 2)], hsem, T.sem.ls, pid, rid, f["full"])
-        return ones_of(f["full"])
-
-    tot += pair(0, T.sem.hp0)
-    wait("g", t_ds)
+    wait("g", t_ds0)
     if helper is None:
-        tot += far_targets(g, T, topo, info, rank, T.sem.ls)
+        tot += targets(g, T, topo, info, rank, range(4), f["off"], T.sem.ls)
     else:
         g.remote_dma(T.DS[:, 0:128], T.DS[:, 0:128], T.sem.hd, T.sem.ls, pid, rid, f["full"])
         tot += ones_of(f["full"])
-    tot += pair(2, T.sem.hp1)
-    ms = split(f["on"], 4)
-    tr = []
-    for k in range(4, 7):
-        tr.append(RemoteDMATransfer(src=T.DS[:, 32 * k:32 * k + 32], dst=T.DL[:, 32 * rank:32 * rank + 32],
-                                    dst_ids=[dst_id(topo, info[f["order"][k]]["core"])], dma_engine_mask=ms[k - 4], remote_sem=T.sem.dl))
-        tot += ones_of(ms[k - 4])
-    g.remote_dma_fused(tr, local_sem=T.sem.ls)
+    for k, hsem in ((0, T.sem.hp0), (2, T.sem.hp1)):
+        wait("g", t_g[k], t_g[k + 1])
+        if helper is None:
+            tot += far_pair(g, T, topo, info, rank, k, T.sem.ls)
+        else:
+            g.remote_dma(T.G[:, CAP * k:CAP * (k + 2)], T.G[:, CAP * k:CAP * (k + 2)], hsem, T.sem.ls, pid, rid, f["full"])
+            tot += ones_of(f["full"])
+    wait("g", t_ds1)
+    tot += targets(g, T, topo, info, rank, range(4, 7), f["on"], T.sem.ls)
     wait("g", t_g[4], t_g[5])
     ms = split(f["on"], 2)
+    land = T.comb[:, R + CAP * rank:R + CAP * (rank + 1)]
     tr = []
     for k in range(4, 6):
-        tr.append(RemoteDMATransfer(src=T.G[:, CAP * k:CAP * (k + 1)], dst=T.comb[:, R + CAP * rank:R + CAP * (rank + 1)],
+        tr.append(RemoteDMATransfer(src=T.G[:, CAP * k:CAP * (k + 1)], dst=land,
                                     dst_ids=[dst_id(topo, info[f["order"][k]]["core"])], dma_engine_mask=ms[k - 4], remote_sem=T.sem.dat))
     g.remote_dma_fused(tr, local_sem=T.sem.ls)
     tot += ones_of(f["on"])
     wait("g", t_g[6])
     rd, pd, _e = topo.addr(info[f["order"][6]]["core"])
-    g.remote_dma(T.comb[:, R + CAP * rank:R + CAP * (rank + 1)], T.G[:, CAP * 6:CAP * 7], T.sem.dat, T.sem.ls, pd, rd, f["on"])
+    g.remote_dma(land, T.G[:, CAP * 6:CAP * 7], T.sem.dat, T.sem.ls, pd, rd, f["on"])
     tot += ones_of(f["on"])
 
     ndl = ndat = 0
@@ -522,7 +496,7 @@ def member_program(g, core, T, topo, info, rank):
             ndl += ones_of(h["on"]) // 4
             ndat += ones_of(h["on"]) // (2 if k < 6 else 1)
     V.wait_ge(T.sem.dl, ndl)
-    wait("v", t_ds)
+    wait("v", t_ds1)
     vt(T.DX[:, 0:128], T.DL[:, 0:128], T.DL[:, 128:256], A.max)
     drain("v")
     vt(T.DX[:, 128:192], T.DX[:, 0:64], T.DX[:, 64:128], A.max)
@@ -531,42 +505,50 @@ def member_program(g, core, T, topo, info, rank):
     drain("v")
     vt(T.DX[:, 224:256], T.DX[:, 192:224], T.Cc[:, 0:32], A.max)
     drain("v")
-    op("v", V.tensor_copy(T.OT[:], T.DX[:, 224:256]))
+    vc(T.OT[:], T.DX[:, 224:256])
     drain("v")
-    wait("v", t_iw)
-    op("v", V.tensor_copy(T.IW[:].indirect(T.OT[:]), T.SV[:]))
+    wait("v", t_iw, t_sv)
+    vc(T.IW[:].indirect(T.OT[:]), T.SV[:])
     t_is = cut("v")
     wait("p", t_is)
-    t_iu = []
-    t_ip = []
-    for h in range(2):
-        t_ip.append(rewrap(T.b3 if h == 0 else T.b4, T.IW, CAP + 4096 * h, CAP + 4096 * (h + 1), T.BS))
-    for h in range(2):
-        wait("v", t_ip[h])
-        vt(T.IF[:, 256 * h:256 * h + 256], (T.b3 if h == 0 else T.b4)[:, 0:256], T.Cc[:, 256 * h:256 * h + 256], A.max)
+    tbank = [T.b3, T.b4]
+    rbank = [T.b0, T.b1, T.b2, T.b5]
+    t_iu, t_r, t_h, t_c = [], [], [], []
+    for h in range(5):
+        if h < 4:
+            if h >= 2:
+                wait("p", t_c[h - 2])
+            t_h.append(turn(tbank[h % 2], T.IW, CAP + 2048 * h, 16))
+            wait("s", t_h[h])
+            sc(T.TI[:, 256 * h:256 * h + 256], tbank[h % 2][:, 0:256])
+            t_c.append(cut("s"))
+        if h > 0:
+            wait("p", t_c[h - 1])
+            t_r.append(back(rbank[h - 1], T.TI, 256 * (h - 1)))
+    for h in range(4):
+        c0, c1 = 128 * h, 128 * h + 128
+        wait("v", t_r[h])
+        vt(T.IF[:, c0:c1], rbank[h][:, 0:128], T.Cc[:, c0:c1], A.max)
         drain("v")
-        op("v", V.tensor_copy(T.IU[:, 256 * h:256 * h + 256], T.IF[:, 256 * h:256 * h + 256]))
+        vc(T.IU[:, c0:c1], T.IF[:, c0:c1])
         t_iu.append(drain("v"))
 
     V.wait_ge(T.sem.dat, ndat)
     wait("v", t_g[7])
     S.wait_ge(T.sem.dat, ndat)
-    wait("s", t_g[7], t_iu[1])
-    wins = T.comb[:]
-    cs = 0
-    stores = []
+    wait("s", t_g[7], t_iu[2], t_iu[3])
+    c0 = 0
     for n in CH:
         for q in ("v", "s"):
-            a = cs if q == "v" else cs + 4096
-            i = wins.indirect(T.IU[:, a // 16:(a + n) // 16])
+            a = c0 if q == "v" else c0 + R // 2
+            i = T.comb[:].indirect(T.IU[:, a // 16:(a + n) // 16])
             if q == "v":
-                op(q, V.tensor_copy(T.YB[:, a:a + n], i))
+                vc(T.YB[:, a:a + n], i)
             else:
-                op(q, S.activation(T.YB[:, a:a + n], i, F.Copy))
-            t = cut(q)
-            wait("y", t)
-            stores.append(dmas("y", [(T.y[:, a:a + n], T.YB[:, a:a + n])]))
-        cs += n
+                sc(T.YB[:, a:a + n], i)
+            wait("y", cut(q))
+            dmas("y", [(T.y[:, a:a + n], T.YB[:, a:a + n])])
+        c0 += n
     g.wait_ge(T.sem.ls, tot)
     for t in allt:
         if t[2] not in waited:

@@ -6,25 +6,26 @@ SIM = 112
 MSG = 80
 B0 = 1025
 WW = B0 + N * CAP + 15
-CH = [256, 512, 768, 1024, 768, 512, 256]
+CH = [256, 768, 1024, 1024, 768, 256]
 
-SCRATCH = {"L": ("sbuf", [128, N * MSG], "bfloat16")}
-for _n, _w in (("comb", R + N * CAP), ("G", N * CAP), ("YB", R), ("Wd", WW), ("IW", CAP + R), ("Z", 512), ("Id", 128), ("Ih", 128),
-               ("Tri", 128), ("One", 128), ("M2", 8), ("Ex", 512), ("Wt", 1024), ("Rs", 512), ("E1", 32), ("SV", 512), ("KI", 32),
-               ("KZ", 32), ("U0", 1024), ("U1", 1024), ("M", 512), ("MS", 512), ("AM", 512), ("S0", 512), ("S1", 512), ("TB", 1024),
-               ("TI", 1024)):
+SCRATCH = {}
+for _n, _w in (("L", 4 * MSG), ("comb", R + N * CAP), ("G", N * CAP), ("Q", CAP), ("YB", R), ("Wd", WW), ("IW", CAP + R), ("Z", 512),
+               ("Id", 128), ("Ih", 128), ("Tri", 128), ("One", 128), ("Kc", 256), ("Ex", 512), ("Wt", 1024), ("Rs", 512), ("E1", 16),
+               ("E4", 4), ("Ed", 128), ("Ee", 128), ("SV", 512), ("KI", 32), ("KZ", 32), ("U", 1024), ("M", 512), ("MS", 512),
+               ("S0", 512), ("SM", 128), ("SR", 256), ("RL", 64), ("DP", 1024), ("A1", 256), ("TI", 1024)):
     SCRATCH[_n] = ("sbuf", [128, _w], "bfloat16")
-for _n, _w in (("PF", 32), ("DK", 128), ("J128", 128), ("Cc", 512), ("KF", 16), ("XF", 128), ("OF0", 64), ("OF1", 64), ("DS", 256),
-               ("DL", 256), ("DX", 256), ("IF", 512)):
+for _n, _w in (("PF", 32), ("DK", 128), ("D4", 128), ("J128", 128), ("Cc", 512), ("KF", 16), ("XF", 128), ("OF", 64), ("DX", 32),
+               ("IF", 512)):
     SCRATCH[_n] = ("sbuf", [128, _w], "float32")
 for _n, _w in (("PI", 8), ("NT", 32), ("NU", 32), ("XC", 64), ("XL", 64), ("XH", 64)):
     SCRATCH[_n] = ("sbuf", [128, _w], "int32")
-for _n, _w in (("OU0", 64), ("OU1", 64), ("SO", 256), ("OT", 32), ("IU", 512)):
+for _n, _w in (("OU", 64), ("SO", 256), ("OT", 32), ("IV", 512), ("IU", 512)):
     SCRATCH[_n] = ("sbuf", [128, _w], "uint16")
 for _k in range(8):
     SCRATCH["b%d" % _k] = ("psum", [128, 512], "float32")
-NSEM = 138
-SEMAPHORES = ["la1", "la2", "dl", "dat", "hl", "hp0", "hp1", "hd", "lls", "ls"] + ["s%d" % k for k in range(NSEM)]
+NSEM = 100
+SEMAPHORES = ["la0", "la1", "la2", "la3", "n0", "n1", "f0", "f1", "rf", "dl", "hp0", "hp1", "hq", "dat", "iu0", "iu1", "lls", "ls"]
+SEMAPHORES += ["s%d" % k for k in range(NSEM)]
 
 
 def ones_of(mask):
@@ -39,100 +40,124 @@ def split(mask, k):
 
 def layout(T, topo):
     cores = T.cores
-    info = []
-    for r in range(N):
-        c = cores[r]
-        here = [x for x in range(N) if topo.chip(cores[x]) == topo.chip(c)]
-        away = [x for x in range(N) if x not in here]
-        info.append({"core": c, "here": here, "away": away, "i": here.index(r), "helper": None})
-    for r in range(N):
-        f = info[r]
-        far = [cores[x] for x in f["away"]]
-        if all(topo.may_write(f["core"], x) for x in far):
-            continue
-        used = [i["helper"] for i in info]
-        free = [h for h in range(SIM) if topo.chip(h) == topo.chip(f["core"]) and h not in cores
-                and h not in used and all(topo.may_write(h, x) for x in far)]
-        f["helper"] = free[0]
-    for f in info:
-        i, n = f["i"], len(f["here"])
-        f["order"] = [f["away"][(i + k) % n] for k in range(n)] + [f["here"][(i + k) % n] for k in range(1, n)] + [f["here"][i]]
-        far = cores[f["away"][0]]
-        nb = cores[f["here"][(i + 1) % n]]
-        on = topo.mask(f["core"], nb)
-        src = f["core"] if f["helper"] is None else f["helper"]
-        f["off"] = topo.mask(src, far)
-        f["on"] = (on & ~f["off"]) if f["helper"] is None else on
-        f["full"] = on
-    return info
+    lay = {"all": [], "full": {}, "off": {}, "on": {}, "chip": {}}
+    for name in ("near", "far", "port", "second", "inv", "here", "away", "own"):
+        lay[name] = [None] * N
+    for ch in sorted(set(topo.chip(c) for c in cores)):
+        here = [r for r in range(N) if topo.chip(cores[r]) == ch]
+        away = [r for r in range(N) if r not in here]
+        allc = [c for c in range(SIM) if topo.chip(c) == ch]
+        port = [c for c in allc if all(topo.may_write(c, cores[x]) for x in away)]
+        idle = [c for c in allc if c not in cores]
+        fport = [c for c in idle if c in port]
+        frest = [c for c in idle if c not in port]
+        rport = [c for c in cores if c in port]
+        for k, a in enumerate(here):
+            c = cores[a]
+            if c in port:
+                lay["near"][a], lay["port"][a] = frest.pop(0), c
+            else:
+                lay["near"][a], lay["port"][a], lay["second"][a] = c, fport.pop(0), rport.pop(0)
+            lay["inv"][a], lay["here"][a], lay["away"][a], lay["own"][a] = idle[k], here, away, k
+        for k, a in enumerate(away):
+            lay["far"][a] = port[k]
+        for c in allc:
+            full = topo.mask(c, [x for x in allc if x != c][0])
+            off = topo.mask(c, cores[away[0]])
+            lay["full"][c] = full
+            lay["off"][c] = off if c in port else 0
+            lay["on"][c] = full & ~off if c in port else full
+            lay["chip"][c] = here
+        lay["all"] += allc
+    return lay
+
+
+def slot_calls(lay, cores, a, near):
+    home = cores[a]
+    s, z = (0, "n") if near else (128, "f")
+
+    def inv(bs, c):
+        out = []
+        for b in bs:
+            lb = 0 if (b in lay["here"][a]) == near else 512
+            if lay["inv"][b] != c:
+                out.append((lay["inv"][b], "DP", lb + 64 * a, "dl"))
+        return out
+    if near:
+        c = lay["near"][a]
+        full = lay["full"][c]
+        far = (home, "SR", s, z + "0") if home != c else (lay["port"][a], "RL", 0, "rf")
+        one = [(0, full, [far])]
+        if home != c:
+            m = split(full, 2)
+            two = [(1, m[0], [(home, "SR", s + 64, z + "1")]), (1, m[1], inv(lay["here"][a], c))]
+        else:
+            two = [(1, full, inv(lay["here"][a], c))]
+        return [one, two]
+    c = lay["far"][a]
+    one = [(0, lay["off"][c], [(home, "SR", s, z + "0")]), (0, lay["on"][c], inv(lay["away"][a], c))]
+    two = [(1, lay["off"][c], [(home, "SR", s + 64, z + "1")])]
+    return [one, two]
+
+
+def home_call(lay, cores, a):
+    return [(1, lay["on"][cores[a]], [(lay["inv"][b], "DP", 512 + 64 * a, "dl") for b in lay["here"][a]])]
+
+
+def forward_call(lay, a):
+    return [(0, lay["off"][lay["port"][a]], [(lay["inv"][b], "DP", 512 + 64 * a, "dl") for b in lay["away"][a]])]
+
+
+def data_calls(lay, cores, a):
+    k, c, p, p2 = lay["own"][a], cores[a], lay["port"][a], lay["second"][a]
+    fa = [lay["away"][a][(k + i) % 4] for i in range(4)]
+    ne = [lay["here"][a][(k + i) % 4] for i in range(1, 4)]
+    mf = split(lay["off"][p], 2)
+    mo = split(lay["on"][c], 2)
+    if p == c:
+        far = [(p, None, [0, 1], mf, fa[0:2]), (p, None, [2, 3], mf, fa[2:4])]
+    else:
+        far = [(p, "hp0", [0, 1], mf, fa[0:2]), (p, "hp1", [2], [lay["off"][p]], fa[2:3]), (p2, "hq", [3], [lay["off"][p2]], fa[3:4])]
+    return far + [(c, None, [4, 5], mo, ne[0:2]), (c, None, [6], [lay["on"][c]], ne[2:3])]
+
+
+def arrivals(lay, cores, core):
+    got = {}
+
+    def add(s, n):
+        got[s] = got.get(s, 0) + n
+    for a in range(N):
+        for call in slot_calls(lay, cores, a, True) + slot_calls(lay, cores, a, False) + [forward_call(lay, a), home_call(lay, cores, a)]:
+            for _h, m, ds in call:
+                for d in ds:
+                    if d[0] == core:
+                        add(d[3], ones_of(m))
+        for _c, _s, _p, ms, bs in data_calls(lay, cores, a):
+            for m, b in zip(ms, bs):
+                if cores[b] == core:
+                    add("dat", ones_of(m))
+        f = lay["full"][cores[a]]
+        if lay["port"][a] == core and cores[a] != core:
+            add("hp0", ones_of(f))
+            add("hp1", ones_of(f) // 2)
+        if lay["second"][a] == core:
+            add("hq", ones_of(f) // 2)
+    return got
 
 
 def rank_program(g, core, T, topo):
-    info = layout(T, topo)
-    rank = T.rank_of(core)
-    if rank is None:
-        for r in range(N):
-            if info[r]["helper"] == core:
-                helper_program(g, T, topo, info, r)
+    cores = T.cores
+    lay = layout(T, topo)
+    if core not in lay["all"]:
         return
-    member_program(g, core, T, topo, info, rank)
-
-
-def dst_id(topo, c):
-    rid, pid, _e = topo.addr(c)
-    return DstId(rid=rid, pnc=pid)
-
-
-def far_pair(g, T, topo, info, r, k, lsem):
-    f = info[r]
-    ms = split(f["off"], 2)
-    tr = []
-    for j in range(2):
-        d = info[f["order"][k + j]]["core"]
-        tr.append(RemoteDMATransfer(src=T.G[:, CAP * (k + j):CAP * (k + j + 1)], dst=T.comb[:, R + CAP * r:R + CAP * (r + 1)],
-                                    dst_ids=[dst_id(topo, d)], dma_engine_mask=ms[j], remote_sem=T.sem.dat))
-    g.remote_dma_fused(tr, local_sem=lsem)
-    return ones_of(f["off"])
-
-
-def targets(g, T, topo, info, r, ks, mask, lsem):
-    f = info[r]
-    ms = split(mask, 4)
-    tr = []
-    for j, k in enumerate(ks):
-        d = info[f["order"][k]]["core"]
-        tr.append(RemoteDMATransfer(src=T.DS[:, 32 * k:32 * k + 32], dst=T.DL[:, 32 * r:32 * r + 32],
-                                    dst_ids=[dst_id(topo, d)], dma_engine_mask=ms[j], remote_sem=T.sem.dl))
-    g.remote_dma_fused(tr, local_sem=lsem)
-    return ones_of(mask) // 4 * len(ks)
-
-
-def far_list(T, topo, info, r, slot):
-    f = info[r]
-    to = [info[x]["core"] for x in f["away"]]
-    z = 4 + f["i"]
-    return RemoteDMATransfer(src=T.L[:, MSG * slot:MSG * slot + MSG], dsts=[T.L[:, MSG * z:MSG * z + MSG] for _ in to],
-                             dst_ids=[dst_id(topo, c) for c in to], dma_engine_mask=f["off"], remote_sem=T.sem.la2)
-
-
-def helper_program(g, T, topo, info, r):
-    f = info[r]
-    g.wait_ge(T.sem.hl, ones_of(f["full"]))
-    g.remote_dma_fused([far_list(T, topo, info, r, f["i"])], local_sem=T.sem.ls)
-    tot = ones_of(f["off"])
-    g.wait_ge(T.sem.hd, ones_of(f["full"]))
-    tot += targets(g, T, topo, info, r, range(4), f["off"], T.sem.ls)
-    g.wait_ge(T.sem.hp0, ones_of(f["full"]))
-    tot += far_pair(g, T, topo, info, r, 0, T.sem.ls)
-    g.wait_ge(T.sem.hp1, ones_of(f["full"]))
-    tot += far_pair(g, T, topo, info, r, 2, T.sem.ls)
-    g.wait_ge(T.sem.ls, tot)
-
-
-def member_program(g, core, T, topo, info, rank):
-    f = info[rank]
-    own = f["i"]
-    helper = f["helper"]
+    rank = T.rank_of(core)
+    got = arrivals(lay, cores, core)
+    here = lay["chip"][core]
+    near = core in lay["near"]
+    a = lay["near"].index(core) if near else lay["far"].index(core)
+    order = lay["away"][a] + lay["here"][a]
+    b_inv = lay["inv"].index(core) if core in lay["inv"] else None
+    a_port = lay["port"].index(core) if core in lay["port"] else None
     V, S, P, Y = g.vector, g.scalar, g.tensor, g.sync
     queues = {"v": V, "s": S, "p": P, "y": Y, "g": g}
     st = {"n": 0}
@@ -166,6 +191,10 @@ def member_program(g, core, T, topo, info, rank):
             waited[t[2]] = True
             queues[q].wait_ge(t[0], t[1])
 
+    def arrive(q, name):
+        if got.get(name, 0):
+            queues[q].wait_ge(T.sem[name], got[name])
+
     def drain(q):
         t = cut(q)
         wait(q, t)
@@ -185,17 +214,17 @@ def member_program(g, core, T, topo, info, rank):
         else:
             op("v", V.tensor_scalar(out, in0, s1, s2, o0, o1))
 
-    def vt(out, a, b, o):
-        op("v", V.tensor_tensor(out, a, b, o))
+    def vt(out, x, y, o):
+        op("v", V.tensor_tensor(out, x, y, o))
 
-    def vc(out, a):
-        op("v", V.tensor_copy(out, a))
+    def vc(out, x):
+        op("v", V.tensor_copy(out, x))
 
-    def sc(out, a):
-        op("s", S.activation(out, a, F.Copy))
+    def sc(out, x):
+        op("s", S.activation(out, x, F.Copy))
 
-    def mm(out, l, r, a, b):
-        op("p", P.matmul(out, l, r, a, b))
+    def mm(out, l, r, x, y):
+        op("p", P.matmul(out, l, r, x, y))
 
     def pi(k):
         return T.PI[:, k:k + 1]
@@ -203,353 +232,397 @@ def member_program(g, core, T, topo, info, rank):
     def pf(k):
         return T.PF[:, k:k + 1]
 
-    t_nat = dmas("y", [(T.NT[:, 0:16], T.src[:]), (T.NT[:, 16:32], T.dst[:])])
-    t_xc = dmas("s", [(T.XC[0::4, :], T.src[:]), (T.XC[1::4, :], T.src[:]), (T.XC[2::4, :], T.dst[:]), (T.XC[3::4, :], T.dst[:])])
+    def ident(c):
+        rid, pid, _e = topo.addr(c)
+        return DstId(rid=rid, pnc=pid)
+
+    tot = [0]
+
+    def fused(parts, lsem):
+        tr = []
+        for src, m, ds in parts:
+            tr.append(RemoteDMATransfer(src=src, dsts=[d[1] for d in ds], dst_ids=[ident(d[0]) for d in ds], dma_engine_mask=m,
+                                        remote_sem=T.sem[ds[0][2]]))
+            tot[0] += ones_of(m)
+        g.remote_dma_fused(tr, local_sem=lsem)
+
+    def slots(call, src):
+        fused([(src[h], m, [(d[0], T[d[1]][:, d[2]:d[2] + 64], d[3]) for d in ds]) for h, m, ds in call], T.sem.ls)
+
+    def blocks(x, call, src):
+        land = T.comb[:, R + CAP * x:R + CAP * (x + 1)]
+        fused([(s, m, [(cores[b], land, "dat")]) for s, m, b in zip(src, call[3], call[4])], T.sem.ls)
+
+    def block(n):
+        return T.G[:, CAP * n:CAP * (n + 1)]
+
+    if rank is not None:
+        t_nat = dmas("y", [(T.NT[:, 0:16], T.src[:]), (T.NT[:, 16:32], T.dst[:])])
+        t_xc = dmas("s", [(T.XC[0::4, :], T.src[:]), (T.XC[1::4, :], T.src[:]), (T.XC[2::4, :], T.dst[:]), (T.XC[3::4, :], T.dst[:])])
 
     op("g", g.iota(T.PI[:, 0:1], [[1, 1]], 0, 1))
     t_i0 = cut("g")
     op("g", g.iota(T.DK[:], [[1, 128]], 0, -1, allow_small_or_imprecise_dtypes=True))
     t_i1 = cut("g")
-    op("g", g.iota(T.Cc[:], [[16, 512]], 0, 0, allow_small_or_imprecise_dtypes=True))
-    op("g", g.iota(T.J128[:], [[1, 128]], 0, 0, allow_small_or_imprecise_dtypes=True))
+    op("g", g.iota(T.Cc[:, 0:64], [[16, 64]], 0, 0, allow_small_or_imprecise_dtypes=True))
+    if rank is not None:
+        op("g", g.iota(T.D4[:], [[0, 8], [4, 16]], 0, -1, allow_small_or_imprecise_dtypes=True))
     t_i2 = cut("g")
+    if b_inv is not None:
+        op("g", g.iota(T.Cc[:, 64:512], [[16, 448]], 1024, 0, allow_small_or_imprecise_dtypes=True))
+        op("g", g.iota(T.J128[:], [[1, 128]], 0, 0, allow_small_or_imprecise_dtypes=True))
+        t_i3 = cut("g")
 
     wait("v", t_i0)
-    vs(pi(5), pi(0), 4, 1, A.logical_shift_right, A.bitwise_and)
-    vs(pi(6), pi(0), 1, None, A.bitwise_and)
-    vs(pi(3), pi(0), 3, None, A.bitwise_and)
+    if rank is not None:
+        vs(pi(5), pi(0), 4, 1, A.logical_shift_right, A.bitwise_and)
+        vs(pi(6), pi(0), 1, None, A.bitwise_and)
+        vs(pi(3), pi(0), 3, None, A.bitwise_and)
     vs(pi(1), pi(0), 15, None, A.bitwise_and)
     vs(pi(2), pi(0), 4, None, A.logical_shift_right)
     vs(pi(4), pi(0), 2, 3, A.logical_shift_right, A.bitwise_and)
-    drain("v")
-    vs(pf(1), pi(5), 0, None, A.is_equal)
-    vs(pf(2), pi(5), 1, None, A.is_equal)
-    vs(pf(3), pi(6), 0, None, A.is_equal)
-    vs(pf(4), pi(6), 1, None, A.is_equal)
-    vs(pf(5), pi(3), 3, 4.0, A.is_equal, A.mult)
     op("v", V.memset(T.Z[:], 0.0))
-    t_z = cut("v")
+    t_z = drain("v")
+    if rank is not None:
+        vs(pf(1), pi(5), 0, None, A.is_equal)
+        vs(pf(2), pi(5), 1, None, A.is_equal)
+        vs(pf(3), pi(6), 0, None, A.is_equal)
+        vs(pf(4), pi(6), 1, None, A.is_equal)
+        vs(pf(5), pi(3), 3, 4.0, A.is_equal, A.mult)
 
-    z = MSG * own
-    wait("v", t_nat)
-    vs(T.NU[:, 0:16], T.NT[:, 0:16], 10, 0xFFF8, A.arith_shift_right, A.bitwise_and)
-    vs(T.NU[:, 16:32], T.NT[:, 16:32], 13, None, A.arith_shift_right)
-    wait("v", t_xc)
-    vs(T.XL[:], T.XC[:], 127, None, A.bitwise_and)
-    vs(T.XH[:], T.XC[:], 7, 63, A.arith_shift_right, A.bitwise_and)
-    wait("v", t_z)
-    drain("v")
-    vt(T.KF[:], T.NU[:, 0:16], T.NU[:, 16:32], A.add)
-    vs(T.XF[:, 0:64], T.XL[:], pf(3), None, A.mult)
-    vs(T.XF[:, 64:128], T.XH[:], pf(4), pf(5), A.mult, A.add)
-    drain("v")
-    vs(T.KI[:, 0:16], T.KF[:], pf(1), None, A.mult)
-    vs(T.KI[:, 16:32], T.KF[:], pf(2), None, A.mult)
-    vt(T.L[:, z + 16:z + 80], T.XF[:, 0:64], T.XF[:, 64:128], A.add)
-    drain("v")
-    op("v", V.transpose(T.KZ[:], T.KI[:]))
-    drain("v")
-    vt(T.L[:, z:z + 16], T.KZ[:, 0:16], T.KZ[:, 16:32], A.add)
-    t_msg = cut("v")
+        z = MSG * lay["own"][rank]
+        wait("v", t_nat)
+        vs(T.NU[:, 0:16], T.NT[:, 0:16], 10, 0xFFF8, A.arith_shift_right, A.bitwise_and)
+        vs(T.NU[:, 16:32], T.NT[:, 16:32], 13, None, A.arith_shift_right)
+        wait("v", t_xc)
+        vs(T.XL[:], T.XC[:], 127, None, A.bitwise_and)
+        vs(T.XH[:], T.XC[:], 7, 63, A.arith_shift_right, A.bitwise_and)
+        drain("v")
+        vt(T.KF[:], T.NU[:, 0:16], T.NU[:, 16:32], A.add)
+        vs(T.XF[:, 0:64], T.XL[:], pf(3), None, A.mult)
+        vs(T.XF[:, 64:128], T.XH[:], pf(4), pf(5), A.mult, A.add)
+        drain("v")
+        vs(T.KI[:, 0:16], T.KF[:], pf(1), None, A.mult)
+        vs(T.KI[:, 16:32], T.KF[:], pf(2), None, A.mult)
+        vt(T.L[:, z + 16:z + 80], T.XF[:, 0:64], T.XF[:, 64:128], A.add)
+        drain("v")
+        op("v", V.transpose(T.KZ[:], T.KI[:]))
+        drain("v")
+        vt(T.L[:, z:z + 16], T.KZ[:, 0:16], T.KZ[:, 16:32], A.add)
+        t_msg = cut("v")
 
-    wait("g", t_msg)
-    near = [info[x]["core"] for x in f["order"][4:7]]
-    mine = T.L[:, z:z + MSG]
-    on = RemoteDMATransfer(src=mine, dsts=[mine] * 3, dst_ids=[dst_id(topo, c) for c in near],
-                           dma_engine_mask=f["on"], remote_sem=T.sem.la1)
-    rid = pid = None
-    if helper is None:
-        g.remote_dma_fused([far_list(T, topo, info, rank, own), on], local_sem=T.sem.lls)
-        nl = ones_of(f["on"]) + ones_of(f["off"])
-    else:
-        rid, pid, _e = topo.addr(helper)
-        g.remote_dma_fused([on], local_sem=T.sem.lls)
-        g.remote_dma(mine, mine, T.sem.hl, T.sem.lls, pid, rid, f["full"])
-        nl = ones_of(f["on"]) + ones_of(f["full"])
-    Y.wait_ge(T.sem.lls, nl)
-    t_tab = dmas("y", [(T.comb[:, 0:R], T.tab[:])])
+        wait("g", t_msg)
+        others = [lay["near"][x] for x in lay["here"][rank]] + [lay["far"][x] for x in lay["away"][rank]]
+        others = [c for c in others if c not in cores] + [c for c in others if c in cores]
+        mine = T.L[:, z:z + MSG]
+        fused([(mine, lay["full"][core], [(c, mine, "la%d" % lay["own"][rank]) for c in others if c != core])], T.sem.lls)
+        Y.wait_ge(T.sem.lls, tot[0])
+        tot[0] = 0
+        t_tab = dmas("y", [(T.comb[:, 0:R], T.tab[:])])
 
     wait("v", t_i1)
     vs(T.Id[:], T.DK[:], 0.0, None, A.is_equal)
     for s in range(4):
         vs(pf(6 + s), pi(4), s, None, A.is_equal)
     vc(pf(0), pi(1))
-    vs(pf(10), pi(1), 0, None, A.is_equal)
-    vs(pf(11), pi(1), 1, None, A.is_equal)
-    vs(pf(12), pi(1), 2, None, A.is_equal)
-    vs(pf(13), pi(1), 3, None, A.is_equal)
+    for k in range(4):
+        vs(pf(10 + k), pi(1), k, None, A.is_equal)
     vs(pf(18), pi(2), 4.0, 64.0, A.mult, A.add)
-    op("v", V.memset(T.One[:], 1.0))
-    op("v", V.memset(T.M2[:], -2.0))
+    op("v", V.memset(T.One[:], 1.0 if near else -1.0))
+    op("v", V.memset(T.Kc[:], -255.0 / 128.0 if near else -2.0))
     op("v", V.memset(T.Rs[:], 1.0))
-    op("v", V.memset(T.E1[:, 16:32], 0.0))
     drain("v")
     for s in range(4):
         vs(T.Ex[:, 128 * s:128 * s + 128], T.DK[:], -4.0 * s, pf(6 + s), A.is_equal, A.mult)
-    for m in range(4):
-        vs(pf(14 + m), pf(18), float(m), pf(11), A.add, A.mult)
     t_pf = cut("v")
-    vs(T.Tri[:], T.DK[:], 0.0, None, A.is_gt)
-    for b in range(8):
-        vs(T.Wt[:, 128 * b:128 * b + 128], T.DK[:], 0.0, 256.0 * (5 + 2 * b), A.is_equal, A.mult)
-    vs(T.Ih[:], T.DK[:], 0.0, 128.0, A.is_equal, A.mult)
     op("v", V.memset(T.Rs[:, 0::64], 0.0))
+    vs(T.Tri[:], T.DK[:], 0.0, -1.0 if near else 1.0, A.is_le, A.mult)
+    for k in range(8):
+        vs(T.Wt[:, 128 * k:128 * k + 128], T.Id[:], 256.0 * (5 + 2 * k), None, A.mult)
     wait("v", t_i2)
     vs(T.Cc[:, 0:64], T.Cc[:, 0:64], pf(0), None, A.add)
-    vs(T.E1[:, 0:8], T.One[:, 0:8], pf(10), None, A.mult)
-    vs(T.E1[:, 8:16], T.One[:, 0:8], pf(11), None, A.mult)
-    vc(T.E1[:, 16 + rank:17 + rank], pf(12))
-    vc(T.E1[:, 24 + rank:25 + rank], pf(13))
+    for k in range(4):
+        vc(T.E4[:, k:k + 1], pf(10 + k))
     t_const = drain("v")
 
+    def late_constants():
+        if rank is not None:
+            vs(T.Ed[:], T.D4[:], 0.0, None, A.is_equal)
+            vs(T.Ee[:], T.D4[:], -1.0, 128.0, A.is_equal, A.mult)
+            drain("v")
+            vt(T.Ed[:], T.Ed[:], T.Ee[:], A.add)
+        if b_inv is not None:
+            vs(T.Ih[:], T.Id[:], 128.0, None, A.mult)
+            vs(T.E1[:, 0:8], T.One[:, 0:8], 0.0, pf(10), A.mult, A.add)
+            vs(T.E1[:, 8:16], T.One[:, 0:8], 0.0, pf(11), A.mult, A.add)
+            for m in range(4):
+                vs(pf(14 + m), pf(18), float(m), pf(11), A.add, A.mult)
+        return drain("v")
+
+    if rank is None:
+        t_late = late_constants()
+
     wait("s", t_z)
-    c0 = 0
+    c0 = B0
     while c0 < WW:
         n = min(512, WW - c0)
         sc(T.Wd[:, c0:c0 + n], T.Z[:, 0:n])
         c0 += n
     t_wd = cut("s")
-    wait("s", t_pf, t_i2)
-    op("s", S.activation(T.Cc[:, 64:512], T.Cc[:, 64:512], F.Identity, bias=pf(0)))
-    for m in range(4):
-        op("s", S.activation(T.SV[:, 128 * m:128 * m + 128], T.J128[:], F.Identity, bias=pf(14 + m), scale=pf(10)))
-    t_sv = cut("s")
 
-    banks = [(T.b0, T.b1, T.b2), (T.b5, T.b6, T.b7)]
-    t_u = None
-    for pc in range(2):
-        bK, bA, bX = banks[pc]
-        Sb, OF, OU, U = (T.S0, T.OF0, T.OU0, T.U0) if pc == 0 else (T.S1, T.OF1, T.OU1, T.U1)
-        wait("p", t_msg, t_pf)
-        if pc == 0:
-            P.wait_ge(T.sem.la1, sum(ones_of(info[x]["on"]) for x in f["order"][4:7]))
-        else:
-            P.wait_ge(T.sem.la2, sum(ones_of(info[x]["off"]) for x in f["away"]))
-        for sl in range(4):
-            zl = MSG * (4 * pc + sl)
-            mm(bK[:, 16 * sl:16 * sl + 16], T.Id[:], T.L[:, zl:zl + 16], True, True)
-        t_k = cut("p")
-        if pc == 1:
-            wait("p", t_u)
-        for sl in range(4):
-            zl = MSG * (4 * pc + sl)
-            bu = T.b3 if sl < 2 else T.b4
-            for s in range(4):
-                o = 256 * (sl % 2) + 64 * s
-                mm(bu[:, o:o + 64], T.Ex[:, 128 * s:128 * s + 128], T.L[:, zl + 16:zl + 80], True, True)
-        t_up = cut("p")
-        wait("s", t_up)
-        sc(U[:, 0:512], T.b3[:])
-        sc(U[:, 512:1024], T.b4[:])
-        t_u = cut("s")
-        for blk in (range(0, 6) if pc == 0 else range(6, 16)):
-            sc(T.IW[:, CAP + 512 * blk:CAP + 512 * blk + 512], T.Z[:])
-        t_iw = cut("s")
-        wait("v", t_k)
-        for b in range(8):
-            vs(T.M[:, 64 * b:64 * b + 64], bK[:, 0:64], float(8 * rank + f["order"][b]), None, A.is_equal)
-        t_m = drain("v")
-        op("v", V.tensor_tensor_scan(Sb[:], T.Rs[:], T.M[:], 0.0, A.mult, A.add))
-        t_s = drain("v")
-        vt(T.MS[:], T.M[:], Sb[:], A.mult)
-        t_ms = cut("v")
-        wait("p", t_const, t_m)
-        for b in range(8):
-            mm(bX[:, 0:64], T.Wt[:, 128 * b:128 * b + 128], T.M[:, 64 * b:64 * b + 64], b == 0, False)
-        wait("p", t_s)
-        cut("p")
-        mm(bA[:, 0:8], T.One[:], T.M2[:], True, False)
-        if pc == 1:
-            mm(bA[:, 0:8], T.One[:], T.S0[:, 63::64], False, False)
-        mm(bA[:, 0:8], T.Tri[:], Sb[:, 63::64], False, True)
-        t_a = cut("p")
-        wait("p", t_ms)
-        for b in range(8):
-            mm(bX[:, 0:64], T.Id[:], T.MS[:, 64 * b:64 * b + 64], False, False)
-        wait("v", t_a)
-        for b in range(8):
-            vs(T.AM[:, 64 * b:64 * b + 64], bK[:, 0:64], float(8 * rank + f["order"][b]), bA[:, b:b + 1], A.is_equal, A.mult)
-        t_am = cut("v")
-        wait("p", t_am)
-        for b in range(8):
-            mm(bX[:, 0:64], T.Id[:], T.AM[:, 64 * b:64 * b + 64], False, b == 7)
-        t_x = cut("p")
-        wait("v", t_x)
-        vt(OF[:], bX[:, 0:64], T.Cc[:, 0:64], A.max)
-        drain("v")
-        vc(OU[:], OF[:])
-        drain("v")
-        wait("v", t_u, t_wd)
-        vc(T.Wd[:].indirect(OU[:]), U[:])
-        t_sc = drain("v") if pc == 0 else cut("v")
+    bK, bX, bP = T.b0, T.b1, (T.b2, T.b5)
 
-    def turn(bank, W, c0, n):
-        for q in range(16):
-            mm(bank[:, q:16 * n:16], W[:, c0 + q:c0 + 2048:16], T.E1[:, 0:n], True, True)
-        return cut("p")
-
-    def back(bank, tb, c):
-        mm(bank[:, 0:128], tb[:, c:c + 128], T.Id[:], True, False)
-        mm(bank[:, 0:128], tb[:, c + 128:c + 256], T.Ih[:], False, True)
-        return cut("p")
-
-    t_g = {}
-    win = T.comb[:, 0:R]
-
-    def gath(q, k):
-        o = T.comb[:, R + CAP * rank:R + CAP * (rank + 1)] if k == 7 else T.G[:, CAP * k:CAP * (k + 1)]
-        i = win.indirect(T.SO[:, 32 * k:32 * k + 32])
-        if q == "v":
-            vc(o, i)
-        else:
-            sc(o, i)
-        t_g[k] = cut(q)
-
-    wait("p", t_sc)
-    t_h0 = turn(T.b0, T.Wd, B0, 32)
-    wait("v", t_h0)
-    vc(T.TB[:, 0:256], T.b0[:, 0:256])
-    t_t0 = cut("v")
-    wait("p", t_t0)
-    t_s0 = back(T.b1, T.TB, 0)
-    wait("s", t_t0)
-    sc(T.TB[:, 256:512], T.b0[:, 256:512])
-    t_t1 = cut("s")
-    wait("p", t_t1)
-    t_d0 = back(T.b2, T.TB, 256)
-    t_h1 = turn(T.b5, T.Wd, B0 + 2048, 32)
-    wait("v", t_s0)
-    vc(T.SO[:, 0:128], T.b1[:, 0:128])
-    t_so0 = drain("v")
-    wait("v", t_tab)
-    gath("v", 1)
-    wait("v", t_h1)
-    vc(T.TB[:, 512:768], T.b5[:, 0:256])
-    t_t2 = cut("v")
-    gath("v", 3)
-    wait("p", t_t2)
-    t_s1 = back(T.b6, T.TB, 512)
-    wait("s", t_d0)
-    sc(T.DS[:, 0:128], T.b2[:, 0:128])
-    t_ds0 = cut("s")
-    wait("s", t_so0, t_tab)
-    gath("s", 0)
-    gath("s", 2)
-    wait("s", t_t2)
-    sc(T.TB[:, 768:1024], T.b5[:, 256:512])
-    t_t3 = cut("s")
-    wait("p", t_t3)
-    t_d1 = back(T.b7, T.TB, 768)
-    wait("v", t_s1)
-    vc(T.SO[:, 128:256], T.b6[:, 0:128])
-    t_so1 = drain("v")
-    wait("s", t_d1)
-    sc(T.DS[:, 128:256], T.b7[:, 0:128])
-    sc(T.DL[:, 32 * rank:32 * rank + 32], T.b7[:, 96:128])
-    t_ds1 = cut("s")
-    wait("s", t_so1)
-    gath("s", 4)
-    gath("s", 6)
-    gath("v", 5)
-    gath("v", 7)
-
-    tot = 0
-    wait("g", t_ds0)
-    if helper is None:
-        tot += targets(g, T, topo, info, rank, range(4), f["off"], T.sem.ls)
-    else:
-        g.remote_dma(T.DS[:, 0:128], T.DS[:, 0:128], T.sem.hd, T.sem.ls, pid, rid, f["full"])
-        tot += ones_of(f["full"])
-    for k, hsem in ((0, T.sem.hp0), (2, T.sem.hp1)):
-        wait("g", t_g[k], t_g[k + 1])
-        if helper is None:
-            tot += far_pair(g, T, topo, info, rank, k, T.sem.ls)
-        else:
-            g.remote_dma(T.G[:, CAP * k:CAP * (k + 2)], T.G[:, CAP * k:CAP * (k + 2)], hsem, T.sem.ls, pid, rid, f["full"])
-            tot += ones_of(f["full"])
-    wait("g", t_ds1)
-    tot += targets(g, T, topo, info, rank, range(4, 7), f["on"], T.sem.ls)
-    wait("g", t_g[4], t_g[5])
-    ms = split(f["on"], 2)
-    land = T.comb[:, R + CAP * rank:R + CAP * (rank + 1)]
-    tr = []
-    for k in range(4, 6):
-        tr.append(RemoteDMATransfer(src=T.G[:, CAP * k:CAP * (k + 1)], dst=land,
-                                    dst_ids=[dst_id(topo, info[f["order"][k]]["core"])], dma_engine_mask=ms[k - 4], remote_sem=T.sem.dat))
-    g.remote_dma_fused(tr, local_sem=T.sem.ls)
-    tot += ones_of(f["on"])
-    wait("g", t_g[6])
-    rd, pd, _e = topo.addr(info[f["order"][6]]["core"])
-    g.remote_dma(land, T.G[:, CAP * 6:CAP * 7], T.sem.dat, T.sem.ls, pd, rd, f["on"])
-    tot += ones_of(f["on"])
-
-    ndl = ndat = 0
-    for x in range(N):
+    def keys(x):
+        sl = lay["own"][x]
         if x == rank:
-            continue
-        h = info[x]
-        k = h["order"].index(rank)
-        if k < 4:
-            ndl += ones_of(h["off"]) // 4
-            ndat += ones_of(h["off"]) // 2
+            wait("p", t_msg)
         else:
-            ndl += ones_of(h["on"]) // 4
-            ndat += ones_of(h["on"]) // (2 if k < 6 else 1)
-    V.wait_ge(T.sem.dl, ndl)
-    wait("v", t_ds1)
-    vt(T.DX[:, 0:128], T.DL[:, 0:128], T.DL[:, 128:256], A.max)
-    drain("v")
-    vt(T.DX[:, 128:192], T.DX[:, 0:64], T.DX[:, 64:128], A.max)
-    drain("v")
-    vt(T.DX[:, 192:224], T.DX[:, 128:160], T.DX[:, 160:192], A.max)
-    drain("v")
-    vt(T.DX[:, 224:256], T.DX[:, 192:224], T.Cc[:, 0:32], A.max)
-    drain("v")
-    vc(T.OT[:], T.DX[:, 224:256])
-    drain("v")
-    wait("v", t_iw, t_sv)
-    vc(T.IW[:].indirect(T.OT[:]), T.SV[:])
-    t_is = cut("v")
-    wait("p", t_is)
-    tbank = [T.b3, T.b4]
-    rbank = [T.b0, T.b1, T.b2, T.b5]
-    t_iu, t_r, t_h, t_c = [], [], [], []
-    for h in range(5):
-        if h < 4:
-            if h >= 2:
-                wait("p", t_c[h - 2])
-            t_h.append(turn(tbank[h % 2], T.IW, CAP + 2048 * h, 16))
-            wait("s", t_h[h])
-            sc(T.TI[:, 256 * h:256 * h + 256], tbank[h % 2][:, 0:256])
-            t_c.append(cut("s"))
-        if h > 0:
-            wait("p", t_c[h - 1])
-            t_r.append(back(rbank[h - 1], T.TI, 256 * (h - 1)))
-    for h in range(4):
-        c0, c1 = 128 * h, 128 * h + 128
-        wait("v", t_r[h])
-        vt(T.IF[:, c0:c1], rbank[h][:, 0:128], T.Cc[:, c0:c1], A.max)
-        drain("v")
-        vc(T.IU[:, c0:c1], T.IF[:, c0:c1])
-        t_iu.append(drain("v"))
+            P.wait_ge(T.sem["la%d" % sl], ones_of(lay["full"][cores[x]]))
+        mm(bK[:, 16 * sl:16 * sl + 16], T.Id[:], T.L[:, MSG * sl:MSG * sl + 16], True, True)
 
-    V.wait_ge(T.sem.dat, ndat)
-    wait("v", t_g[7])
-    S.wait_ge(T.sem.dat, ndat)
-    wait("s", t_g[7], t_iu[2], t_iu[3])
-    c0 = 0
-    for n in CH:
-        for q in ("v", "s"):
-            a = c0 if q == "v" else c0 + R // 2
-            i = T.comb[:].indirect(T.IU[:, a // 16:(a + n) // 16])
+    def planes(x):
+        sl = lay["own"][x]
+        bu, zl = (T.b3 if sl < 2 else T.b4), MSG * sl
+        for s in range(4):
+            o = 256 * (sl % 2) + 64 * s
+            mm(bu[:, o:o + 64], T.Ex[:, 128 * s:128 * s + 128], T.L[:, zl + 16:zl + 80], True, True)
+
+    wait("p", t_pf)
+    for k in range(2):
+        mm(bP[k][:, 0:256], T.One[:], T.Kc[:], True, False)
+    if rank is not None:
+        keys(rank)
+        planes(rank)
+    cut("p")
+    rest = [x for x in here if x != rank]
+    for x in rest:
+        keys(x)
+    t_k = cut("p")
+    for x in rest[:2]:
+        planes(x)
+    wait("p", t_const)
+    wait("v", t_k)
+    t_b, t_h, t_sm = [], [], []
+    for h in range(2):
+        c0 = 256 * h
+        for k in range(4 * h, 4 * h + 4):
+            vs(T.M[:, 64 * k:64 * k + 64], bK[:, 0:64], float(8 * a + order[k]), None, A.is_equal)
+        wait("p", drain("v"))
+        op("v", V.tensor_tensor_scan(T.S0[:, c0:c0 + 256], T.Rs[:, c0:c0 + 256], T.M[:, c0:c0 + 256], 0.0, A.mult, A.add))
+        mm(bP[h][:, 0:256], T.Tri[:], T.M[:, c0:c0 + 256], False, False)
+        wait("p", cut("v"))
+        mm(bP[h][:, 0:256], T.One[:], T.S0[:, c0:c0 + 256], False, True)
+        t_b.append(cut("p"))
+        if h == 0:
+            for x in rest[2:]:
+                planes(x)
+            wait("s", cut("p"))
+            sc(T.U[:, 0:512], T.b3[:])
+            sc(T.U[:, 512:1024], T.b4[:])
+            t_u = cut("s")
+    for k in range(8):
+        mm(bX[:, 0:64], T.Wt[:, 128 * k:128 * k + 128], T.M[:, 64 * k:64 * k + 64], k == 0, False)
+    for h in range(2):
+        c0 = 256 * h
+        wait("v", t_b[h])
+        vt(T.MS[:, c0:c0 + 256], T.M[:, c0:c0 + 256], bP[h][:, 0:256], A.mult)
+        wait("p", cut("v"))
+        for k in range(4 * h, 4 * h + 4):
+            mm(bX[:, 0:64], T.Id[:], T.MS[:, 64 * k:64 * k + 64], False, k == 7)
+    wait("v", cut("p"))
+    vt(T.OF[:], bX[:, 0:64], T.Cc[:, 0:64], A.max)
+    drain("v")
+    vc(T.OU[:], T.OF[:])
+    drain("v")
+    wait("v", t_u, t_wd)
+    vc(T.Wd[:].indirect(T.OU[:]), T.U[:])
+    t_sc = drain("v")
+
+    bT = (T.b6, T.b7)
+    wait("p", t_sc)
+    for h in range(2):
+        for q in range(16):
+            c0 = B0 + 2048 * h + q
+            mm(bT[h][:, 4 * q:4 * q + 4], T.Wd[:, c0:c0 + 2033:16], T.E4[:], True, True)
+        t_h.append(cut("p"))
+    calls = slot_calls(lay, cores, a, near)
+    src = [T.SM[:, 0:64], T.SM[:, 64:128]]
+    t_own, t_dp = [], None
+    for h in range(2):
+        wait("v", t_h[h])
+        vc(src[h], bT[h][:, 0:64])
+        t_sm.append(cut("v"))
+        if near and rank is not None:
+            vc(T.SR[:, 64 * h:64 * h + 64], bT[h][:, 0:64])
+            t_own.append(cut("v"))
+        if b_inv is not None and ((b_inv in lay["away"][a]) == (h == 0)):
+            lb = 0 if (b_inv in lay["here"][a]) == near else 512
+            vc(T.DP[:, lb + 64 * a:lb + 64 * a + 64], bT[h][:, 0:64])
+            t_dp = cut("v")
+    for h in range(2):
+        wait("g", t_sm[h])
+        slots(calls[h], src)
+    if a_port is not None:
+        own = rank is not None
+        arrive("g", "n0" if own else "rf")
+        slots(forward_call(lay, a_port), [T.SR[:, 0:64] if own else T.RL[:]])
+    if rank is not None:
+        arrive("g", "f1")
+        slots(home_call(lay, cores, rank), [None, T.SR[:, 192:256]])
+
+    if b_inv is not None:
+        k = lay["own"][b_inv]
+        for blk in range(16):
+            sc(T.IW[:, CAP + 512 * blk:CAP + 512 * blk + 512], T.Z[:])
+        wait("s", t_i3, t_late)
+        op("s", S.activation(T.Cc[:, 64:512], T.Cc[:, 64:512], F.Identity, bias=pf(0)))
+        for m in range(4):
+            op("s", S.activation(T.SV[:, 128 * m:128 * m + 128], T.J128[:], F.Identity, bias=pf(14 + m), scale=pf(10)))
+        t_iw = cut("s")
+        arrive("p", "dl")
+        wait("p", t_dp, t_late)
+        for i in range(2):
+            mm(T.b0[:, 0:32], T.DP[:, 512 * i + 2:512 * i + 512:4], T.Id[:, 32 * k:32 * k + 32], i == 0, False)
+            mm(T.b0[:, 0:32], T.DP[:, 512 * i + 3:512 * i + 512:4], T.Ih[:, 32 * k:32 * k + 32], False, i == 1)
+        wait("v", cut("p"))
+        vt(T.DX[:], T.b0[:, 0:32], T.Cc[:, 0:32], A.max)
+        drain("v")
+        vc(T.OT[:], T.DX[:])
+        drain("v")
+        wait("v", t_iw)
+        vc(T.IW[:].indirect(T.OT[:]), T.SV[:])
+        wait("p", cut("v"))
+        tb, rb = (T.b3, T.b4), (T.b1, T.b2, T.b5, T.b6)
+        t_c, t_r, t_iu = [], [], []
+        for m in range(2):
+            for n in (2 * m, 2 * m + 1):
+                if m == 1:
+                    wait("p", t_c[n - 2])
+                c0 = CAP + 2048 * n
+                for q in range(16):
+                    mm(tb[n % 2][:, q:256:16], T.IW[:, c0 + q:c0 + 2048:16], T.E1[:], True, True)
+                wait("s", cut("p"))
+                sc(T.TI[:, 256 * n:256 * n + 256], tb[n % 2][:, 0:256])
+                t_c.append(cut("s"))
+            for n in (2 * m, 2 * m + 1):
+                wait("p", t_c[n])
+                c0 = 256 * n
+                mm(rb[n][:, 0:128], T.TI[:, c0:c0 + 128], T.Id[:], True, False)
+                mm(rb[n][:, 0:128], T.TI[:, c0 + 128:c0 + 256], T.Ih[:], False, True)
+                t_r.append(cut("p"))
+        for n in range(4):
+            c0 = 128 * n
+            wait("v", t_r[n])
+            vt(T.IF[:, c0:c0 + 128], rb[n][:, 0:128], T.Cc[:, c0:c0 + 128], A.max)
+            drain("v")
+            vc(T.IV[:, c0:c0 + 128], T.IF[:, c0:c0 + 128])
+            t_iu.append(cut("v"))
+        if a_port is not None:
+            for call in data_calls(lay, cores, a_port)[0:2]:
+                arrive("g", call[1])
+                blocks(a_port, call, [block(n) for n in call[2]])
+        for n in range(2):
+            wait("g", t_iu[2 * n], t_iu[2 * n + 1])
+            fused([(T.IV[:, 256 * n:256 * n + 256], lay["on"][core], [(cores[b_inv], T.IU[:, 256 * n:256 * n + 256], "iu%d" % n)])],
+                  T.sem.ls)
+
+    if rank is not None:
+        t_late = late_constants()
+        dc = data_calls(lay, cores, rank)
+        dest = [b for call in dc for b in call[4]] + [rank]
+        home = lay["away"][rank] + lay["here"][rank]
+        t_g = {}
+
+        def gath(q, n):
+            k = home.index(dest[n])
+            o = T.comb[:, R + CAP * rank:R + CAP * (rank + 1)] if n == 7 else block(n)
+            i = T.comb[:, 0:R].indirect(T.SO[:, 32 * k:32 * k + 32])
             if q == "v":
-                vc(T.YB[:, a:a + n], i)
+                vc(o, i)
             else:
-                sc(T.YB[:, a:a + n], i)
-            wait("y", cut(q))
-            dmas("y", [(T.y[:, a:a + n], T.YB[:, a:a + n])])
-        c0 += n
-    g.wait_ge(T.sem.ls, tot)
+                sc(o, i)
+            t_g[n] = cut(q)
+
+        b1, b2 = (T.b0, T.b3), (T.b1, T.b4)
+        t_1, t_2, t_so = [], [], []
+
+        def first(h):
+            arrive("p", "n%d" % h)
+            arrive("p", "f%d" % h)
+            if t_own:
+                wait("p", t_own[h])
+            for i in range(2):
+                c0 = 128 * i + 64 * h
+                mm(b1[h][0:64, 0:128], T.SR[:, c0:c0 + 64], T.Id[:], i == 0, i == 1)
+            t_1.append(cut("p"))
+
+        def second(h):
+            wait("v", t_1[h])
+            vc(T.A1[0:64, 128 * h:128 * h + 128], b1[h][0:64, 0:128])
+            wait("p", cut("v"), t_late)
+            mm(b2[h][:, 0:128], T.Ed[0:64, :], T.A1[0:64, 128 * h:128 * h + 128], True, True)
+            t_2.append(cut("p"))
+
+        def third(h):
+            wait("v", t_2[h])
+            vc(T.SO[:, 128 * h:128 * h + 128], b2[h][:, 0:128])
+            t_so.append(drain("v"))
+
+        first(0)
+        second(0)
+        third(0)
+        wait("v", t_tab)
+        gath("v", 1)
+        wait("s", t_so[0], t_tab)
+        gath("s", 0)
+        gath("s", 2)
+        first(1)
+        second(1)
+        gath("v", 3)
+        third(1)
+        wait("s", t_so[1])
+        gath("s", 4)
+        gath("s", 6)
+        gath("v", 5)
+        gath("v", 7)
+
+        if a_port is None:
+            p, p2, full = lay["port"][rank], lay["second"][rank], lay["full"][core]
+            wait("g", t_g[0], t_g[1])
+            pair = T.G[:, 0:2 * CAP]
+            fused([(pair, full, [(p, pair, "hp0")])], T.sem.ls)
+            wait("g", t_g[2], t_g[3])
+            m = split(full, 2)
+            fused([(block(2), m[0], [(p, block(2), "hp1")]), (block(3), m[1], [(p2, T.Q[:], "hq")])], T.sem.ls)
+        for call in dc:
+            if call[1] is None:
+                wait("g", *[t_g[n] for n in call[2]])
+                blocks(rank, call, [block(n) for n in call[2]])
+        for x in here:
+            if lay["second"][x] == core:
+                arrive("g", "hq")
+                blocks(x, data_calls(lay, cores, x)[2], [T.Q[:]])
+
+        maker = lay["inv"][rank]
+        for q in ("v", "s"):
+            queues[q].wait_ge(T.sem.iu0, ones_of(lay["on"][maker]))
+            arrive(q, "dat")
+            wait(q, t_g[7])
+        c0 = 0
+        for n in CH:
+            for q in ("v", "s"):
+                c = c0 if q == "v" else c0 + n
+                if c0 == R // 2:
+                    queues[q].wait_ge(T.sem.iu1, ones_of(lay["on"][maker]))
+                i = T.comb[:].indirect(T.IU[:, c // 16:(c + n) // 16])
+                if q == "v":
+                    vc(T.YB[:, c:c + n], i)
+                else:
+                    sc(T.YB[:, c:c + n], i)
+                wait("y", cut(q))
+            dmas("y", [(T.y[:, c0:c0 + 2 * n], T.YB[:, c0:c0 + 2 * n])])
+            c0 += 2 * n
+    g.wait_ge(T.sem.ls, tot[0])
     for t in allt:
         if t[2] not in waited:
             wait("g", t)

@@ -3,28 +3,32 @@ from concourse.mybir import AluOpType as A, ActivationFunctionType as F
 
 N, R, CAP = 8, 8192, 512
 SIM = 112
+DB = 640
 MSG = 80
-B0 = 1025
+B0 = 1281
 WW = B0 + N * CAP + 15
+WG = B0 + 2560
 CH = [256, 768, 1024, 1024, 768, 256]
+IUP = 4
 
 SCRATCH = {}
-for _n, _w in (("L", 4 * MSG), ("comb", R + N * CAP), ("G", N * CAP), ("Q", CAP), ("YB", R), ("Wd", WW), ("IW", CAP + R), ("Z", 512),
+for _n, _w in (("L", 4 * MSG), ("comb", R + N * CAP), ("G", N * CAP), ("Q", CAP), ("YB", R), ("Wd", WW), ("IW", DB + R), ("Z", 512),
                ("Id", 128), ("Ih", 128), ("Tri", 128), ("One", 128), ("Kc", 256), ("Ex", 512), ("Wt", 1024), ("Rs", 512), ("E1", 16),
-               ("E4", 4), ("Ed", 128), ("Ee", 128), ("SV", 512), ("KI", 32), ("KZ", 32), ("U", 1024), ("M", 512), ("MS", 512),
+               ("E4", 4), ("Ed", 128), ("Ee", 128), ("SV", 512), ("U", 1024), ("M", 512), ("MS", 512),
                ("S0", 512), ("SM", 128), ("SR", 256), ("RL", 64), ("DP", 1024), ("A1", 256), ("TI", 1024)):
     SCRATCH[_n] = ("sbuf", [128, _w], "bfloat16")
-for _n, _w in (("PF", 32), ("DK", 128), ("D4", 128), ("J128", 128), ("Cc", 512), ("KF", 16), ("XF", 128), ("OF", 64), ("DX", 32),
+for _n, _w in (("PF", 32), ("DK", 128), ("D4", 128), ("DQ", 128), ("J128", 128), ("Cc", 64), ("Ci", 512), ("OF", 64), ("DX", 32),
                ("IF", 512)):
     SCRATCH[_n] = ("sbuf", [128, _w], "float32")
-for _n, _w in (("PI", 8), ("NT", 32), ("NU", 32), ("XC", 64), ("XL", 64), ("XH", 64)):
+for _n, _w in (("PI", 8), ("NT", 32), ("NX", 32), ("NU", 32), ("XC", 64), ("XL", 64)):
     SCRATCH[_n] = ("sbuf", [128, _w], "int32")
 for _n, _w in (("OU", 64), ("SO", 256), ("OT", 32), ("IV", 512), ("IU", 512)):
     SCRATCH[_n] = ("sbuf", [128, _w], "uint16")
 for _k in range(8):
     SCRATCH["b%d" % _k] = ("psum", [128, 512], "float32")
-NSEM = 100
-SEMAPHORES = ["la0", "la1", "la2", "la3", "n0", "n1", "f0", "f1", "rf", "dl", "hp0", "hp1", "hq", "dat", "iu0", "iu1", "lls", "ls"]
+NSEM = 118
+SEMAPHORES = ["la0", "la1", "la2", "la3", "n0", "n1", "f0", "f1", "rf", "dl", "hp0", "hp1", "hp2", "hq", "dat", "iu0", "iu1", "iu2",
+              "iu3", "lls", "ls"]
 SEMAPHORES += ["s%d" % k for k in range(NSEM)]
 
 
@@ -51,13 +55,15 @@ def layout(T, topo):
         idle = [c for c in allc if c not in cores]
         fport = [c for c in idle if c in port]
         frest = [c for c in idle if c not in port]
-        rport = [c for c in cores if c in port]
+        rport = [c for c in cores if c in port and topo.chip(c) == ch]
         for k, a in enumerate(here):
             c = cores[a]
             if c in port:
                 lay["near"][a], lay["port"][a] = frest.pop(0), c
             else:
-                lay["near"][a], lay["port"][a], lay["second"][a] = c, fport.pop(0), rport.pop(0)
+                lay["near"][a], lay["port"][a] = c, fport.pop(0)
+                if not fport:
+                    lay["second"][a] = rport[-1]
             lay["inv"][a], lay["here"][a], lay["away"][a], lay["own"][a] = idle[k], here, away, k
         for k, a in enumerate(away):
             lay["far"][a] = port[k]
@@ -86,18 +92,15 @@ def slot_calls(lay, cores, a, near):
     if near:
         c = lay["near"][a]
         full = lay["full"][c]
-        far = (home, "SR", s, z + "0") if home != c else (lay["port"][a], "RL", 0, "rf")
-        one = [(0, full, [far])]
+        m = split(full, 2)
         if home != c:
-            m = split(full, 2)
-            two = [(1, m[0], [(home, "SR", s + 64, z + "1")]), (1, m[1], inv(lay["here"][a], c))]
-        else:
-            two = [(1, full, inv(lay["here"][a], c))]
-        return [one, two]
+            return [[(0, full, [(home, "SR", s, z + "0")])],
+                    [(1, m[0], [(home, "SR", s + 64, z + "1")]), (1, m[1], inv(lay["here"][a], c))]]
+        return [[(0, full, [(lay["port"][a], "RL", 0, "rf")])], [(1, full, inv(lay["here"][a], c))]]
     c = lay["far"][a]
-    one = [(0, lay["off"][c], [(home, "SR", s, z + "0")]), (0, lay["on"][c], inv(lay["away"][a], c))]
+    one = [(0, lay["off"][c], [(home, "SR", s, z + "0")])]
     two = [(1, lay["off"][c], [(home, "SR", s + 64, z + "1")])]
-    return [one, two]
+    return [one, two, [(0, lay["on"][c], inv(lay["away"][a], c))]]
 
 
 def home_call(lay, cores, a):
@@ -109,15 +112,13 @@ def forward_call(lay, a):
 
 
 def data_calls(lay, cores, a):
-    k, c, p, p2 = lay["own"][a], cores[a], lay["port"][a], lay["second"][a]
+    k, c, p = lay["own"][a], cores[a], lay["port"][a]
     fa = [lay["away"][a][(k + i) % 4] for i in range(4)]
     ne = [lay["here"][a][(k + i) % 4] for i in range(1, 4)]
-    mf = split(lay["off"][p], 2)
     mo = split(lay["on"][c], 2)
-    if p == c:
-        far = [(p, None, [0, 1], mf, fa[0:2]), (p, None, [2, 3], mf, fa[2:4])]
-    else:
-        far = [(p, "hp0", [0, 1], mf, fa[0:2]), (p, "hp1", [2], [lay["off"][p]], fa[2:3]), (p2, "hq", [3], [lay["off"][p2]], fa[3:4])]
+    via = [p, p, p, lay["second"][a] or p]
+    sems = [None] * 4 if p == c else ["hp0", "hp1", "hp2", "hq"]
+    far = [(via[i], sems[i], [i], [lay["off"][via[i]]], [fa[i]]) for i in range(4)]
     return far + [(c, None, [4, 5], mo, ne[0:2]), (c, None, [6], [lay["on"][c]], ne[2:3])]
 
 
@@ -139,8 +140,9 @@ def arrivals(lay, cores, core):
         f = lay["full"][cores[a]]
         if lay["port"][a] == core and cores[a] != core:
             add("hp0", ones_of(f))
-            add("hp1", ones_of(f) // 2)
-        if lay["second"][a] == core:
+            add("hp1", ones_of(f))
+            add("hp2", ones_of(f) // 2)
+        if cores[a] != core and data_calls(lay, cores, a)[3][0] == core:
             add("hq", ones_of(f) // 2)
     return got
 
@@ -220,11 +222,17 @@ def rank_program(g, core, T, topo):
     def vc(out, x):
         op("v", V.tensor_copy(out, x))
 
+    def vm(out, c):
+        op("v", V.memset(out, c))
+
     def sc(out, x):
         op("s", S.activation(out, x, F.Copy))
 
     def mm(out, l, r, x, y):
         op("p", P.matmul(out, l, r, x, y))
+
+    def iota(out, pattern, cm):
+        op("g", g.iota(out, pattern, 0, cm, allow_small_or_imprecise_dtypes=True))
 
     def pi(k):
         return T.PI[:, k:k + 1]
@@ -257,58 +265,53 @@ def rank_program(g, core, T, topo):
         return T.G[:, CAP * n:CAP * (n + 1)]
 
     if rank is not None:
-        t_nat = dmas("y", [(T.NT[:, 0:16], T.src[:]), (T.NT[:, 16:32], T.dst[:])])
-        t_xc = dmas("s", [(T.XC[0::4, :], T.src[:]), (T.XC[1::4, :], T.src[:]), (T.XC[2::4, :], T.dst[:]), (T.XC[3::4, :], T.dst[:])])
+        t_nat, t_xc = [], []
+        for i, q, x in ((0, "y", T.src), (1, "s", T.dst)):
+            t_nat.append(dmas(q, [(T.NT[i::2, 16 * h:16 * h + 16], x[8 * h:8 * h + 8, :]) for h in range(2)]))
+        for i, q, x in ((0, "y", T.src), (1, "s", T.dst)):
+            t_xc.append(dmas(q, [(T.XC[32 * j:32 * j + 32, :], x[:]) for j in (i, i + 2)]))
 
-    op("g", g.iota(T.PI[:, 0:1], [[1, 1]], 0, 1))
+    iota(T.DK[:], [[1, 128]], -1)
     t_i0 = cut("g")
-    op("g", g.iota(T.DK[:], [[1, 128]], 0, -1, allow_small_or_imprecise_dtypes=True))
+    op("g", g.iota(T.PI[:, 0:1], [[1, 1]], 0, 1))
+    iota(T.DQ[:], [[4, 4], [16, 2], [32, 16]], -1)
+    iota(T.Cc[:], [[16, 64]], 1)
     t_i1 = cut("g")
-    op("g", g.iota(T.Cc[:, 0:64], [[16, 64]], 0, 0, allow_small_or_imprecise_dtypes=True))
     if rank is not None:
-        op("g", g.iota(T.D4[:], [[0, 8], [4, 16]], 0, -1, allow_small_or_imprecise_dtypes=True))
+        iota(T.D4[:], [[0, 8], [4, 16]], -1)
     t_i2 = cut("g")
     if b_inv is not None:
-        op("g", g.iota(T.Cc[:, 64:512], [[16, 448]], 1024, 0, allow_small_or_imprecise_dtypes=True))
-        op("g", g.iota(T.J128[:], [[1, 128]], 0, 0, allow_small_or_imprecise_dtypes=True))
+        iota(T.Ci[:], [[16, 512]], 0)
+        iota(T.J128[:], [[1, 128]], 0)
         t_i3 = cut("g")
 
+    vm(T.Z[:], 0.0)
+    t_z = cut("v")
+    if rank is not None:
+        vm(T.PF[0:96, 5:6], 0.0)
+        vm(T.PF[96:128, 5:6], 5.0)
+    vm(T.One[:], 1.0 if near else -1.0)
     wait("v", t_i0)
-    if rank is not None:
-        vs(pi(5), pi(0), 4, 1, A.logical_shift_right, A.bitwise_and)
-        vs(pi(6), pi(0), 1, None, A.bitwise_and)
-        vs(pi(3), pi(0), 3, None, A.bitwise_and)
-    vs(pi(1), pi(0), 15, None, A.bitwise_and)
-    vs(pi(2), pi(0), 4, None, A.logical_shift_right)
-    vs(pi(4), pi(0), 2, 3, A.logical_shift_right, A.bitwise_and)
-    op("v", V.memset(T.Z[:], 0.0))
-    t_z = drain("v")
-    if rank is not None:
-        vs(pf(1), pi(5), 0, None, A.is_equal)
-        vs(pf(2), pi(5), 1, None, A.is_equal)
-        vs(pf(3), pi(6), 0, None, A.is_equal)
-        vs(pf(4), pi(6), 1, None, A.is_equal)
-        vs(pf(5), pi(3), 3, 4.0, A.is_equal, A.mult)
+    vs(T.Id[:], T.DK[:], 0.0, None, A.is_equal)
+    t_id = cut("v")
 
+    if rank is not None:
         z = MSG * lay["own"][rank]
-        wait("v", t_nat)
-        vs(T.NU[:, 0:16], T.NT[:, 0:16], 10, 0xFFF8, A.arith_shift_right, A.bitwise_and)
-        vs(T.NU[:, 16:32], T.NT[:, 16:32], 13, None, A.arith_shift_right)
-        wait("v", t_xc)
-        vs(T.XL[:], T.XC[:], 127, None, A.bitwise_and)
-        vs(T.XH[:], T.XC[:], 7, 63, A.arith_shift_right, A.bitwise_and)
-        drain("v")
-        vt(T.KF[:], T.NU[:, 0:16], T.NU[:, 16:32], A.add)
-        vs(T.XF[:, 0:64], T.XL[:], pf(3), None, A.mult)
-        vs(T.XF[:, 64:128], T.XH[:], pf(4), pf(5), A.mult, A.add)
-        drain("v")
-        vs(T.KI[:, 0:16], T.KF[:], pf(1), None, A.mult)
-        vs(T.KI[:, 16:32], T.KF[:], pf(2), None, A.mult)
-        vt(T.L[:, z + 16:z + 80], T.XF[:, 0:64], T.XF[:, 64:128], A.add)
-        drain("v")
-        op("v", V.transpose(T.KZ[:], T.KI[:]))
-        drain("v")
-        vt(T.L[:, z:z + 16], T.KZ[:, 0:16], T.KZ[:, 16:32], A.add)
+        wait("v", *t_nat)
+        op("v", V.transpose(T.NX[:], T.NT[:]))
+        t_nx = cut("v")
+        wait("v", *t_xc)
+        vs(T.XL[0:64, :], T.XC[0:64, :], 127, None, A.bitwise_and)
+        vs(T.XL[64:128, :], T.XC[64:128, :], 7, 63, A.arith_shift_right, A.bitwise_and)
+        t_xl = cut("v")
+        wait("v", t_nx)
+        vs(T.NU[:, 0:16], T.NX[:, 0::2], 10, 0xFFF8, A.arith_shift_right, A.bitwise_and)
+        vs(T.NU[:, 16:32], T.NX[:, 1::2], 13, None, A.arith_shift_right)
+        t_nu = cut("v")
+        wait("v", t_xl)
+        vs(T.L[:, z + 16:z + 80], T.XL[:], pf(5), None, A.add)
+        wait("v", t_nu)
+        vt(T.L[:, z:z + 16], T.NU[:, 0:16], T.NU[:, 16:32], A.add)
         t_msg = cut("v")
 
         wait("g", t_msg)
@@ -320,41 +323,41 @@ def rank_program(g, core, T, topo):
         tot[0] = 0
         t_tab = dmas("y", [(T.comb[:, 0:R], T.tab[:])])
 
-    wait("v", t_i1)
-    vs(T.Id[:], T.DK[:], 0.0, None, A.is_equal)
-    for s in range(4):
-        vs(pf(6 + s), pi(4), s, None, A.is_equal)
-    vc(pf(0), pi(1))
-    for k in range(4):
-        vs(pf(10 + k), pi(1), k, None, A.is_equal)
-    vs(pf(18), pi(2), 4.0, 64.0, A.mult, A.add)
-    op("v", V.memset(T.One[:], 1.0 if near else -1.0))
-    op("v", V.memset(T.Kc[:], -255.0 / 128.0 if near else -2.0))
-    op("v", V.memset(T.Rs[:], 1.0))
-    drain("v")
-    for s in range(4):
-        vs(T.Ex[:, 128 * s:128 * s + 128], T.DK[:], -4.0 * s, pf(6 + s), A.is_equal, A.mult)
-    t_pf = cut("v")
-    op("v", V.memset(T.Rs[:, 0::64], 0.0))
+    iota(T.Wd[:, WG:WW], [[0, WW - WG]], 0)
+    t_wg = cut("g")
+
+    vm(T.Rs[:], 1.0)
+    vm(T.Kc[:], -255.0 / 128.0 if near else -2.0)
     vs(T.Tri[:], T.DK[:], 0.0, -1.0 if near else 1.0, A.is_le, A.mult)
-    for k in range(8):
-        vs(T.Wt[:, 128 * k:128 * k + 128], T.Id[:], 256.0 * (5 + 2 * k), None, A.mult)
-    wait("v", t_i2)
-    vs(T.Cc[:, 0:64], T.Cc[:, 0:64], pf(0), None, A.add)
+    wait("v", t_i1)
+    for s in range(4):
+        vs(T.Ex[:, 128 * s:128 * s + 128], T.DQ[:], float(-s), None, A.is_equal)
+    vs(pi(1), pi(0), 15, None, A.bitwise_and)
+    t_pf = drain("v")
+    vm(T.Rs[:, 0::64], 0.0)
     for k in range(4):
-        vc(T.E4[:, k:k + 1], pf(10 + k))
+        vs(T.E4[:, k:k + 1], pi(1), (0, 2, 1, 3)[k], None, A.is_equal)
     t_const = drain("v")
 
     def late_constants():
         if rank is not None:
+            wait("v", t_i2)
             vs(T.Ed[:], T.D4[:], 0.0, None, A.is_equal)
             vs(T.Ee[:], T.D4[:], -1.0, 128.0, A.is_equal, A.mult)
             drain("v")
             vt(T.Ed[:], T.Ed[:], T.Ee[:], A.add)
         if b_inv is not None:
             vs(T.Ih[:], T.Id[:], 128.0, None, A.mult)
-            vs(T.E1[:, 0:8], T.One[:, 0:8], 0.0, pf(10), A.mult, A.add)
-            vs(T.E1[:, 8:16], T.One[:, 0:8], 0.0, pf(11), A.mult, A.add)
+            vs(pf(10), pi(1), 0, None, A.is_equal)
+            vs(pf(11), pi(1), 1, None, A.is_equal)
+            vs(pi(2), pi(0), 4, None, A.logical_shift_right)
+            vc(pf(0), pi(1))
+            vm(T.Ed[:, 0:8], 0.0)
+            drain("v")
+            vs(pf(18), pi(2), 4.0, 64.0, A.mult, A.add)
+            vs(T.E1[:, 0:8], T.Ed[:, 0:8], pf(10), None, A.add)
+            vs(T.E1[:, 8:16], T.Ed[:, 0:8], pf(11), None, A.add)
+            drain("v")
             for m in range(4):
                 vs(pf(14 + m), pf(18), float(m), pf(11), A.add, A.mult)
         return drain("v")
@@ -362,10 +365,14 @@ def rank_program(g, core, T, topo):
     if rank is None:
         t_late = late_constants()
 
+    wait("s", t_id)
+    for k in range(8):
+        op("s", S.activation(T.Wt[:, 128 * k:128 * k + 128], T.Id[:], F.Copy, scale=256.0 * (6 + 2 * k)))
+    t_wt = cut("s")
     wait("s", t_z)
     c0 = B0
-    while c0 < WW:
-        n = min(512, WW - c0)
+    while c0 < WG:
+        n = min(512, WG - c0)
         sc(T.Wd[:, c0:c0 + n], T.Z[:, 0:n])
         c0 += n
     t_wd = cut("s")
@@ -413,6 +420,9 @@ def rank_program(g, core, T, topo):
         wait("p", cut("v"))
         mm(bP[h][:, 0:256], T.One[:], T.S0[:, c0:c0 + 256], False, True)
         t_b.append(cut("p"))
+        wait("p", t_wt)
+        for k in range(4 * h, 4 * h + 4):
+            mm(bX[:, 0:64], T.Wt[:, 128 * k:128 * k + 128], T.M[:, 64 * k:64 * k + 64], k == 0, False)
         if h == 0:
             for x in rest[2:]:
                 planes(x)
@@ -420,8 +430,6 @@ def rank_program(g, core, T, topo):
             sc(T.U[:, 0:512], T.b3[:])
             sc(T.U[:, 512:1024], T.b4[:])
             t_u = cut("s")
-    for k in range(8):
-        mm(bX[:, 0:64], T.Wt[:, 128 * k:128 * k + 128], T.M[:, 64 * k:64 * k + 64], k == 0, False)
     for h in range(2):
         c0 = 256 * h
         wait("v", t_b[h])
@@ -430,11 +438,11 @@ def rank_program(g, core, T, topo):
         for k in range(4 * h, 4 * h + 4):
             mm(bX[:, 0:64], T.Id[:], T.MS[:, 64 * k:64 * k + 64], False, k == 7)
     wait("v", cut("p"))
-    vt(T.OF[:], bX[:, 0:64], T.Cc[:, 0:64], A.max)
+    vt(T.OF[:], bX[:, 0:64], T.Cc[:], A.max)
     drain("v")
     vc(T.OU[:], T.OF[:])
     drain("v")
-    wait("v", t_u, t_wd)
+    wait("v", t_u, t_wd, t_wg)
     vc(T.Wd[:].indirect(T.OU[:]), T.U[:])
     t_sc = drain("v")
 
@@ -459,9 +467,9 @@ def rank_program(g, core, T, topo):
             lb = 0 if (b_inv in lay["here"][a]) == near else 512
             vc(T.DP[:, lb + 64 * a:lb + 64 * a + 64], bT[h][:, 0:64])
             t_dp = cut("v")
-    for h in range(2):
-        wait("g", t_sm[h])
-        slots(calls[h], src)
+    for call in calls:
+        wait("g", *[t_sm[part[0]] for part in call])
+        slots(call, src)
     if a_port is not None:
         own = rank is not None
         arrive("g", "n0" if own else "rf")
@@ -472,12 +480,14 @@ def rank_program(g, core, T, topo):
 
     if b_inv is not None:
         k = lay["own"][b_inv]
-        for blk in range(16):
-            sc(T.IW[:, CAP + 512 * blk:CAP + 512 * blk + 512], T.Z[:])
+        vm(T.IW[:, DB + R // 2:DB + R], 0.0)
+        t_iv = cut("v")
         wait("s", t_i3, t_late)
-        op("s", S.activation(T.Cc[:, 64:512], T.Cc[:, 64:512], F.Identity, bias=pf(0)))
+        op("s", S.activation(T.Ci[:], T.Ci[:], F.Identity, bias=pf(0)))
         for m in range(4):
             op("s", S.activation(T.SV[:, 128 * m:128 * m + 128], T.J128[:], F.Identity, bias=pf(14 + m), scale=pf(10)))
+        for blk in range(8):
+            sc(T.IW[:, DB + 512 * blk:DB + 512 * blk + 512], T.Z[:])
         t_iw = cut("s")
         arrive("p", "dl")
         wait("p", t_dp, t_late)
@@ -489,41 +499,56 @@ def rank_program(g, core, T, topo):
         drain("v")
         vc(T.OT[:], T.DX[:])
         drain("v")
-        wait("v", t_iw)
+        wait("v", t_iw, t_iv)
         vc(T.IW[:].indirect(T.OT[:]), T.SV[:])
         wait("p", cut("v"))
         tb, rb = (T.b3, T.b4), (T.b1, T.b2, T.b5, T.b6)
         t_c, t_r, t_iu = [], [], []
-        for m in range(2):
-            for n in (2 * m, 2 * m + 1):
-                if m == 1:
-                    wait("p", t_c[n - 2])
-                c0 = CAP + 2048 * n
-                for q in range(16):
-                    mm(tb[n % 2][:, q:256:16], T.IW[:, c0 + q:c0 + 2048:16], T.E1[:], True, True)
-                wait("s", cut("p"))
-                sc(T.TI[:, 256 * n:256 * n + 256], tb[n % 2][:, 0:256])
-                t_c.append(cut("s"))
-            for n in (2 * m, 2 * m + 1):
-                wait("p", t_c[n])
-                c0 = 256 * n
-                mm(rb[n][:, 0:128], T.TI[:, c0:c0 + 128], T.Id[:], True, False)
-                mm(rb[n][:, 0:128], T.TI[:, c0 + 128:c0 + 256], T.Ih[:], False, True)
-                t_r.append(cut("p"))
+
+        def sums(n, q0=0, q1=16):
+            if n >= 2:
+                wait("p", t_c[n - 2])
+            c0 = DB + 2048 * n
+            for q in range(q0, q1):
+                mm(tb[n % 2][:, q:256:16], T.IW[:, c0 + q:c0 + 2048:16], T.E1[:], True, True)
+            if q1 < 16:
+                return
+            wait("s", cut("p"))
+            sc(T.TI[:, 256 * n:256 * n + 256], tb[n % 2][:, 0:256])
+            t_c.append(cut("s"))
+
+        def turned(n):
+            wait("p", t_c[n])
+            c0 = 256 * n
+            mm(rb[n][:, 0:128], T.TI[:, c0:c0 + 128], T.Id[:], True, False)
+            mm(rb[n][:, 0:128], T.TI[:, c0 + 128:c0 + 256], T.Ih[:], False, True)
+            t_r.append(cut("p"))
+
+        sums(0)
+        sums(1, 0, 8)
+        turned(0)
+        sums(1, 8, 16)
+        sums(2, 0, 8)
+        turned(1)
+        sums(2, 8, 16)
+        sums(3)
+        turned(2)
+        turned(3)
         for n in range(4):
             c0 = 128 * n
             wait("v", t_r[n])
-            vt(T.IF[:, c0:c0 + 128], rb[n][:, 0:128], T.Cc[:, c0:c0 + 128], A.max)
+            vt(T.IF[:, c0:c0 + 128], rb[n][:, 0:128], T.Ci[:, c0:c0 + 128], A.max)
             drain("v")
             vc(T.IV[:, c0:c0 + 128], T.IF[:, c0:c0 + 128])
             t_iu.append(cut("v"))
         if a_port is not None:
-            for call in data_calls(lay, cores, a_port)[0:2]:
-                arrive("g", call[1])
-                blocks(a_port, call, [block(n) for n in call[2]])
-        for n in range(2):
-            wait("g", t_iu[2 * n], t_iu[2 * n + 1])
-            fused([(T.IV[:, 256 * n:256 * n + 256], lay["on"][core], [(cores[b_inv], T.IU[:, 256 * n:256 * n + 256], "iu%d" % n)])],
+            for call in data_calls(lay, cores, a_port)[0:4]:
+                if call[0] == core:
+                    arrive("g", call[1])
+                    blocks(a_port, call, [block(n) for n in call[2]])
+        for n in range(IUP):
+            wait("g", t_iu[n])
+            fused([(T.IV[:, 128 * n:128 * n + 128], lay["on"][core], [(cores[b_inv], T.IU[:, 128 * n:128 * n + 128], "iu%d" % n)])],
                   T.sem.ls)
 
     if rank is not None:
@@ -533,15 +558,15 @@ def rank_program(g, core, T, topo):
         home = lay["away"][rank] + lay["here"][rank]
         t_g = {}
 
-        def gath(q, n):
+        def gath(q, n, c0=0, c1=CAP):
             k = home.index(dest[n])
-            o = T.comb[:, R + CAP * rank:R + CAP * (rank + 1)] if n == 7 else block(n)
-            i = T.comb[:, 0:R].indirect(T.SO[:, 32 * k:32 * k + 32])
+            o = T.comb[:, R + CAP * rank + c0:R + CAP * rank + c1] if n == 7 else T.G[:, CAP * n + c0:CAP * n + c1]
+            i = T.comb[:, 0:R].indirect(T.SO[:, 32 * k + c0 // 16:32 * k + c1 // 16])
             if q == "v":
                 vc(o, i)
             else:
                 sc(o, i)
-            t_g[n] = cut(q)
+            t_g.setdefault(n, []).append(cut(q))
 
         b1, b2 = (T.b0, T.b3), (T.b1, T.b4)
         t_1, t_2, t_so = [], [], []
@@ -572,9 +597,10 @@ def rank_program(g, core, T, topo):
         second(0)
         third(0)
         wait("v", t_tab)
-        gath("v", 1)
         wait("s", t_so[0], t_tab)
-        gath("s", 0)
+        for n in range(2):
+            gath("v", n, 0, CAP // 2)
+            gath("s", n, CAP // 2, CAP)
         gath("s", 2)
         first(1)
         second(1)
@@ -587,33 +613,34 @@ def rank_program(g, core, T, topo):
         gath("v", 7)
 
         if a_port is None:
-            p, p2, full = lay["port"][rank], lay["second"][rank], lay["full"][core]
-            wait("g", t_g[0], t_g[1])
-            pair = T.G[:, 0:2 * CAP]
-            fused([(pair, full, [(p, pair, "hp0")])], T.sem.ls)
-            wait("g", t_g[2], t_g[3])
+            p, last_via, full = lay["port"][rank], dc[3][0], lay["full"][core]
+            for n in range(2):
+                wait("g", *t_g[n])
+                fused([(block(n), full, [(p, block(n), "hp%d" % n)])], T.sem.ls)
+            wait("g", *(t_g[2] + t_g[3]))
             m = split(full, 2)
-            fused([(block(2), m[0], [(p, block(2), "hp1")]), (block(3), m[1], [(p2, T.Q[:], "hq")])], T.sem.ls)
+            fused([(block(2), m[0], [(p, block(2), "hp2")]),
+                   (block(3), m[1], [(last_via, block(3) if last_via == p else T.Q[:], "hq")])], T.sem.ls)
         for call in dc:
             if call[1] is None:
-                wait("g", *[t_g[n] for n in call[2]])
+                wait("g", *[t for n in call[2] for t in t_g[n]])
                 blocks(rank, call, [block(n) for n in call[2]])
         for x in here:
             if lay["second"][x] == core:
                 arrive("g", "hq")
-                blocks(x, data_calls(lay, cores, x)[2], [T.Q[:]])
+                blocks(x, data_calls(lay, cores, x)[3], [T.Q[:]])
 
         maker = lay["inv"][rank]
         for q in ("v", "s"):
             queues[q].wait_ge(T.sem.iu0, ones_of(lay["on"][maker]))
             arrive(q, "dat")
-            wait(q, t_g[7])
+            wait(q, *t_g[7])
         c0 = 0
         for n in CH:
             for q in ("v", "s"):
                 c = c0 if q == "v" else c0 + n
-                if c0 == R // 2:
-                    queues[q].wait_ge(T.sem.iu1, ones_of(lay["on"][maker]))
+                if c0 and c0 * IUP % R == 0:
+                    queues[q].wait_ge(T.sem["iu%d" % (c0 * IUP // R)], ones_of(lay["on"][maker]))
                 i = T.comb[:].indirect(T.IU[:, c // 16:(c + n) // 16])
                 if q == "v":
                     vc(T.YB[:, c:c + n], i)

from concourse.bass import DstId, RemoteDMATransfer
from concourse.mybir import AluOpType as A, ActivationFunctionType as F

N, R, CAP = 8, 8192, 512
SIM = 112
DB = 640
MSG = 80
B0 = 1281
WW = B0 + N * CAP + 15
WG = B0 + 2560
CH = [256, 768, 1024, 1024, 768, 256]
IUP = 4

SCRATCH = {}
for _n, _w in (("L", 4 * MSG), ("comb", R + N * CAP), ("G", N * CAP), ("Q", CAP), ("YB", R), ("Wd", WW), ("IW", DB + R), ("Z", 512),
               ("Id", 128), ("Ih", 128), ("Tri", 128), ("One", 128), ("Kc", 256), ("Ex", 512), ("Wt", 1024), ("Rs", 512), ("E1", 16),
               ("E4", 4), ("Ed", 128), ("Ee", 128), ("SV", 512), ("U", 1024), ("M", 512), ("MS", 512),
               ("S0", 512), ("SM", 128), ("SR", 256), ("RL", 64), ("DP", 1024), ("A1", 256), ("TI", 1024)):
    SCRATCH[_n] = ("sbuf", [128, _w], "bfloat16")
for _n, _w in (("PF", 32), ("DK", 128), ("D4", 128), ("DQ", 128), ("J128", 128), ("Cc", 64), ("Ci", 512), ("OF", 64), ("DX", 32),
               ("IF", 512)):
    SCRATCH[_n] = ("sbuf", [128, _w], "float32")
for _n, _w in (("PI", 8), ("NT", 32), ("NX", 32), ("NU", 32), ("XC", 64), ("XL", 64)):
    SCRATCH[_n] = ("sbuf", [128, _w], "int32")
for _n, _w in (("OU", 64), ("SO", 256), ("OT", 32), ("IV", 512), ("IU", 512)):
    SCRATCH[_n] = ("sbuf", [128, _w], "uint16")
for _k in range(8):
    SCRATCH["b%d" % _k] = ("psum", [128, 512], "float32")
NSEM = 118
SEMAPHORES = ["la0", "la1", "la2", "la3", "n0", "n1", "f0", "f1", "rf", "dl", "hp0", "hp1", "hp2", "hq", "dat", "iu0", "iu1", "iu2",
              "iu3", "lls", "ls"]
SEMAPHORES += ["s%d" % k for k in range(NSEM)]


def ones_of(mask):
    return bin(mask).count("1")


def split(mask, k):
    bits = [b for b in range(32) if (mask >> b) & 1]
    n = len(bits) // k
    return [sum(1 << b for b in bits[i * n:(i + 1) * n]) for i in range(k)]


def layout(T, topo):
    cores = T.cores
    lay = {"all": [], "full": {}, "off": {}, "on": {}, "chip": {}}
    for name in ("near", "far", "port", "second", "inv", "here", "away", "own"):
        lay[name] = [None] * N
    for ch in sorted(set(topo.chip(c) for c in cores)):
        here = [r for r in range(N) if topo.chip(cores[r]) == ch]
        away = [r for r in range(N) if r not in here]
        allc = [c for c in range(SIM) if topo.chip(c) == ch]
        port = [c for c in allc if all(topo.may_write(c, cores[x]) for x in away)]
        idle = [c for c in allc if c not in cores]
        fport = [c for c in idle if c in port]
        frest = [c for c in idle if c not in port]
        rport = [c for c in cores if c in port and topo.chip(c) == ch]
        for k, a in enumerate(here):
            c = cores[a]
            if c in port:
                lay["near"][a], lay["port"][a] = frest.pop(0), c
            else:
                lay["near"][a], lay["port"][a] = c, fport.pop(0)
                if not fport:
                    lay["second"][a] = rport[-1]
            lay["inv"][a], lay["here"][a], lay["away"][a], lay["own"][a] = idle[k], here, away, k
        for k, a in enumerate(away):
            lay["far"][a] = port[k]
        for c in allc:
            full = topo.mask(c, [x for x in allc if x != c][0])
            off = topo.mask(c, cores[away[0]])
            lay["full"][c] = full
            lay["off"][c] = off if c in port else 0
            lay["on"][c] = full & ~off if c in port else full
            lay["chip"][c] = here
        lay["all"] += allc
    return lay


def slot_calls(lay, cores, a, near):
    home = cores[a]
    s, z = (0, "n") if near else (128, "f")

    def inv(bs, c):
        out = []
        for b in bs:
            lb = 0 if (b in lay["here"][a]) == near else 512
            if lay["inv"][b] != c:
                out.append((lay["inv"][b], "DP", lb + 64 * a, "dl"))
        return out
    if near:
        c = lay["near"][a]
        full = lay["full"][c]
        m = split(full, 2)
        if home != c:
            return [[(0, full, [(home, "SR", s, z + "0")])],
                    [(1, m[0], [(home, "SR", s + 64, z + "1")]), (1, m[1], inv(lay["here"][a], c))]]
        return [[(0, full, [(lay["port"][a], "RL", 0, "rf")])], [(1, full, inv(lay["here"][a], c))]]
    c = lay["far"][a]
    one = [(0, lay["off"][c], [(home, "SR", s, z + "0")])]
    two = [(1, lay["off"][c], [(home, "SR", s + 64, z + "1")])]
    return [one, two, [(0, lay["on"][c], inv(lay["away"][a], c))]]


def home_call(lay, cores, a):
    return [(1, lay["on"][cores[a]], [(lay["inv"][b], "DP", 512 + 64 * a, "dl") for b in lay["here"][a]])]


def forward_call(lay, a):
    return [(0, lay["off"][lay["port"][a]], [(lay["inv"][b], "DP", 512 + 64 * a, "dl") for b in lay["away"][a]])]


def data_calls(lay, cores, a):
    k, c, p = lay["own"][a], cores[a], lay["port"][a]
    fa = [lay["away"][a][(k + i) % 4] for i in range(4)]
    ne = [lay["here"][a][(k + i) % 4] for i in range(1, 4)]
    mo = split(lay["on"][c], 2)
    via = [p, p, p, lay["second"][a] or p]
    sems = [None] * 4 if p == c else ["hp0", "hp1", "hp2", "hq"]
    far = [(via[i], sems[i], [i], [lay["off"][via[i]]], [fa[i]]) for i in range(4)]
    return far + [(c, None, [4, 5], mo, ne[0:2]), (c, None, [6], [lay["on"][c]], ne[2:3])]


def arrivals(lay, cores, core):
    got = {}

    def add(s, n):
        got[s] = got.get(s, 0) + n
    for a in range(N):
        for call in slot_calls(lay, cores, a, True) + slot_calls(lay, cores, a, False) + [forward_call(lay, a), home_call(lay, cores, a)]:
            for _h, m, ds in call:
                for d in ds:
                    if d[0] == core:
                        add(d[3], ones_of(m))
        for _c, _s, _p, ms, bs in data_calls(lay, cores, a):
            for m, b in zip(ms, bs):
                if cores[b] == core:
                    add("dat", ones_of(m))
        f = lay["full"][cores[a]]
        if lay["port"][a] == core and cores[a] != core:
            add("hp0", ones_of(f))
            add("hp1", ones_of(f))
            add("hp2", ones_of(f) // 2)
        if cores[a] != core and data_calls(lay, cores, a)[3][0] == core:
            add("hq", ones_of(f) // 2)
    return got


def rank_program(g, core, T, topo):
    cores = T.cores
    lay = layout(T, topo)
    if core not in lay["all"]:
        return
    rank = T.rank_of(core)
    got = arrivals(lay, cores, core)
    here = lay["chip"][core]
    near = core in lay["near"]
    a = lay["near"].index(core) if near else lay["far"].index(core)
    order = lay["away"][a] + lay["here"][a]
    b_inv = lay["inv"].index(core) if core in lay["inv"] else None
    a_port = lay["port"].index(core) if core in lay["port"] else None
    V, S, P, Y = g.vector, g.scalar, g.tensor, g.sync
    queues = {"v": V, "s": S, "p": P, "y": Y, "g": g}
    st = {"n": 0}
    cur, last, seen, waited, allt = {}, {}, {}, {}, []

    def new():
        k = st["n"]
        st["n"] = k + 1
        return T.sem["s%d" % k], k

    def op(q, inst):
        if q not in cur:
            sem, k = new()
            cur[q] = [sem, k, 0]
        c = cur[q]
        inst.then_inc(c[0], 1)
        c[2] += 1

    def cut(q):
        if q in cur:
            c = cur.pop(q)
            last[q] = (c[0], c[2], c[1])
            allt.append(last[q])
        return last[q]

    def wait(q, *toks):
        for t in toks:
            if (q, t[2]) in seen:
                continue
            seen[(q, t[2])] = True
            waited[t[2]] = True
            queues[q].wait_ge(t[0], t[1])

    def arrive(q, name):
        if got.get(name, 0):
            queues[q].wait_ge(T.sem[name], got[name])

    def drain(q):
        t = cut(q)
        wait(q, t)
        return t

    def dmas(q, pairs):
        sem, k = new()
        for o, i in pairs:
            queues[q].dma_start(o, i).then_inc(sem, 16)
        t = (sem, 16 * len(pairs), k)
        allt.append(t)
        return t

    def vs(out, in0, s1, s2, o0, o1=None):
        if o1 is None:
            op("v", V.tensor_scalar(out, in0, s1, s2, o0))
        else:
            op("v", V.tensor_scalar(out, in0, s1, s2, o0, o1))

    def vt(out, x, y, o):
        op("v", V.tensor_tensor(out, x, y, o))

    def vc(out, x):
        op("v", V.tensor_copy(out, x))

    def vm(out, c):
        op("v", V.memset(out, c))

    def sc(out, x):
        op("s", S.activation(out, x, F.Copy))

    def mm(out, l, r, x, y):
        op("p", P.matmul(out, l, r, x, y))

    def iota(out, pattern, cm):
        op("g", g.iota(out, pattern, 0, cm, allow_small_or_imprecise_dtypes=True))

    def pi(k):
        return T.PI[:, k:k + 1]

    def pf(k):
        return T.PF[:, k:k + 1]

    def ident(c):
        rid, pid, _e = topo.addr(c)
        return DstId(rid=rid, pnc=pid)

    tot = [0]

    def fused(parts, lsem):
        tr = []
        for src, m, ds in parts:
            tr.append(RemoteDMATransfer(src=src, dsts=[d[1] for d in ds], dst_ids=[ident(d[0]) for d in ds], dma_engine_mask=m,
                                        remote_sem=T.sem[ds[0][2]]))
            tot[0] += ones_of(m)
        g.remote_dma_fused(tr, local_sem=lsem)

    def slots(call, src):
        fused([(src[h], m, [(d[0], T[d[1]][:, d[2]:d[2] + 64], d[3]) for d in ds]) for h, m, ds in call], T.sem.ls)

    def blocks(x, call, src):
        land = T.comb[:, R + CAP * x:R + CAP * (x + 1)]
        fused([(s, m, [(cores[b], land, "dat")]) for s, m, b in zip(src, call[3], call[4])], T.sem.ls)

    def block(n):
        return T.G[:, CAP * n:CAP * (n + 1)]

    if rank is not None:
        t_nat, t_xc = [], []
        for i, q, x in ((0, "y", T.src), (1, "s", T.dst)):
            t_nat.append(dmas(q, [(T.NT[i::2, 16 * h:16 * h + 16], x[8 * h:8 * h + 8, :]) for h in range(2)]))
        for i, q, x in ((0, "y", T.src), (1, "s", T.dst)):
            t_xc.append(dmas(q, [(T.XC[32 * j:32 * j + 32, :], x[:]) for j in (i, i + 2)]))

    iota(T.DK[:], [[1, 128]], -1)
    t_i0 = cut("g")
    op("g", g.iota(T.PI[:, 0:1], [[1, 1]], 0, 1))
    iota(T.DQ[:], [[4, 4], [16, 2], [32, 16]], -1)
    iota(T.Cc[:], [[16, 64]], 1)
    t_i1 = cut("g")
    if rank is not None:
        iota(T.D4[:], [[0, 8], [4, 16]], -1)
    t_i2 = cut("g")
    if b_inv is not None:
        iota(T.Ci[:], [[16, 512]], 0)
        iota(T.J128[:], [[1, 128]], 0)
        t_i3 = cut("g")

    vm(T.Z[:], 0.0)
    t_z = cut("v")
    if rank is not None:
        vm(T.PF[0:96, 5:6], 0.0)
        vm(T.PF[96:128, 5:6], 5.0)
    vm(T.One[:], 1.0 if near else -1.0)
    wait("v", t_i0)
    vs(T.Id[:], T.DK[:], 0.0, None, A.is_equal)
    t_id = cut("v")

    if rank is not None:
        z = MSG * lay["own"][rank]
        wait("v", *t_nat)
        op("v", V.transpose(T.NX[:], T.NT[:]))
        t_nx = cut("v")
        wait("v", *t_xc)
        vs(T.XL[0:64, :], T.XC[0:64, :], 127, None, A.bitwise_and)
        vs(T.XL[64:128, :], T.XC[64:128, :], 7, 63, A.arith_shift_right, A.bitwise_and)
        t_xl = cut("v")
        wait("v", t_nx)
        vs(T.NU[:, 0:16], T.NX[:, 0::2], 10, 0xFFF8, A.arith_shift_right, A.bitwise_and)
        vs(T.NU[:, 16:32], T.NX[:, 1::2], 13, None, A.arith_shift_right)
        t_nu = cut("v")
        wait("v", t_xl)
        vs(T.L[:, z + 16:z + 80], T.XL[:], pf(5), None, A.add)
        wait("v", t_nu)
        vt(T.L[:, z:z + 16], T.NU[:, 0:16], T.NU[:, 16:32], A.add)
        t_msg = cut("v")

        wait("g", t_msg)
        others = [lay["near"][x] for x in lay["here"][rank]] + [lay["far"][x] for x in lay["away"][rank]]
        others = [c for c in others if c not in cores] + [c for c in others if c in cores]
        mine = T.L[:, z:z + MSG]
        fused([(mine, lay["full"][core], [(c, mine, "la%d" % lay["own"][rank]) for c in others if c != core])], T.sem.lls)
        Y.wait_ge(T.sem.lls, tot[0])
        tot[0] = 0
        t_tab = dmas("y", [(T.comb[:, 0:R], T.tab[:])])

    iota(T.Wd[:, WG:WW], [[0, WW - WG]], 0)
    t_wg = cut("g")

    vm(T.Rs[:], 1.0)
    vm(T.Kc[:], -255.0 / 128.0 if near else -2.0)
    vs(T.Tri[:], T.DK[:], 0.0, -1.0 if near else 1.0, A.is_le, A.mult)
    wait("v", t_i1)
    for s in range(4):
        vs(T.Ex[:, 128 * s:128 * s + 128], T.DQ[:], float(-s), None, A.is_equal)
    vs(pi(1), pi(0), 15, None, A.bitwise_and)
    t_pf = drain("v")
    vm(T.Rs[:, 0::64], 0.0)
    for k in range(4):
        vs(T.E4[:, k:k + 1], pi(1), (0, 2, 1, 3)[k], None, A.is_equal)
    t_const = drain("v")

    def late_constants():
        if rank is not None:
            wait("v", t_i2)
            vs(T.Ed[:], T.D4[:], 0.0, None, A.is_equal)
            vs(T.Ee[:], T.D4[:], -1.0, 128.0, A.is_equal, A.mult)
            drain("v")
            vt(T.Ed[:], T.Ed[:], T.Ee[:], A.add)
        if b_inv is not None:
            vs(T.Ih[:], T.Id[:], 128.0, None, A.mult)
            vs(pf(10), pi(1), 0, None, A.is_equal)
            vs(pf(11), pi(1), 1, None, A.is_equal)
            vs(pi(2), pi(0), 4, None, A.logical_shift_right)
            vc(pf(0), pi(1))
            vm(T.Ed[:, 0:8], 0.0)
            drain("v")
            vs(pf(18), pi(2), 4.0, 64.0, A.mult, A.add)
            vs(T.E1[:, 0:8], T.Ed[:, 0:8], pf(10), None, A.add)
            vs(T.E1[:, 8:16], T.Ed[:, 0:8], pf(11), None, A.add)
            drain("v")
            for m in range(4):
                vs(pf(14 + m), pf(18), float(m), pf(11), A.add, A.mult)
        return drain("v")

    if rank is None:
        t_late = late_constants()

    wait("s", t_id)
    for k in range(8):
        op("s", S.activation(T.Wt[:, 128 * k:128 * k + 128], T.Id[:], F.Copy, scale=256.0 * (6 + 2 * k)))
    t_wt = cut("s")
    wait("s", t_z)
    c0 = B0
    while c0 < WG:
        n = min(512, WG - c0)
        sc(T.Wd[:, c0:c0 + n], T.Z[:, 0:n])
        c0 += n
    t_wd = cut("s")

    bK, bX, bP = T.b0, T.b1, (T.b2, T.b5)

    def keys(x):
        sl = lay["own"][x]
        if x == rank:
            wait("p", t_msg)
        else:
            P.wait_ge(T.sem["la%d" % sl], ones_of(lay["full"][cores[x]]))
        mm(bK[:, 16 * sl:16 * sl + 16], T.Id[:], T.L[:, MSG * sl:MSG * sl + 16], True, True)

    def planes(x):
        sl = lay["own"][x]
        bu, zl = (T.b3 if sl < 2 else T.b4), MSG * sl
        for s in range(4):
            o = 256 * (sl % 2) + 64 * s
            mm(bu[:, o:o + 64], T.Ex[:, 128 * s:128 * s + 128], T.L[:, zl + 16:zl + 80], True, True)

    wait("p", t_pf)
    for k in range(2):
        mm(bP[k][:, 0:256], T.One[:], T.Kc[:], True, False)
    if rank is not None:
        keys(rank)
        planes(rank)
    cut("p")
    rest = [x for x in here if x != rank]
    for x in rest:
        keys(x)
    t_k = cut("p")
    for x in rest[:2]:
        planes(x)
    wait("p", t_const)
    wait("v", t_k)
    t_b, t_h, t_sm = [], [], []
    for h in range(2):
        c0 = 256 * h
        for k in range(4 * h, 4 * h + 4):
            vs(T.M[:, 64 * k:64 * k + 64], bK[:, 0:64], float(8 * a + order[k]), None, A.is_equal)
        wait("p", drain("v"))
        op("v", V.tensor_tensor_scan(T.S0[:, c0:c0 + 256], T.Rs[:, c0:c0 + 256], T.M[:, c0:c0 + 256], 0.0, A.mult, A.add))
        mm(bP[h][:, 0:256], T.Tri[:], T.M[:, c0:c0 + 256], False, False)
        wait("p", cut("v"))
        mm(bP[h][:, 0:256], T.One[:], T.S0[:, c0:c0 + 256], False, True)
        t_b.append(cut("p"))
        wait("p", t_wt)
        for k in range(4 * h, 4 * h + 4):
            mm(bX[:, 0:64], T.Wt[:, 128 * k:128 * k + 128], T.M[:, 64 * k:64 * k + 64], k == 0, False)
        if h == 0:
            for x in rest[2:]:
                planes(x)
            wait("s", cut("p"))
            sc(T.U[:, 0:512], T.b3[:])
            sc(T.U[:, 512:1024], T.b4[:])
            t_u = cut("s")
    for h in range(2):
        c0 = 256 * h
        wait("v", t_b[h])
        vt(T.MS[:, c0:c0 + 256], T.M[:, c0:c0 + 256], bP[h][:, 0:256], A.mult)
        wait("p", cut("v"))
        for k in range(4 * h, 4 * h + 4):
            mm(bX[:, 0:64], T.Id[:], T.MS[:, 64 * k:64 * k + 64], False, k == 7)
    wait("v", cut("p"))
    vt(T.OF[:], bX[:, 0:64], T.Cc[:], A.max)
    drain("v")
    vc(T.OU[:], T.OF[:])
    drain("v")
    wait("v", t_u, t_wd, t_wg)
    vc(T.Wd[:].indirect(T.OU[:]), T.U[:])
    t_sc = drain("v")

    bT = (T.b6, T.b7)
    wait("p", t_sc)
    for h in range(2):
        for q in range(16):
            c0 = B0 + 2048 * h + q
            mm(bT[h][:, 4 * q:4 * q + 4], T.Wd[:, c0:c0 + 2033:16], T.E4[:], True, True)
        t_h.append(cut("p"))
    calls = slot_calls(lay, cores, a, near)
    src = [T.SM[:, 0:64], T.SM[:, 64:128]]
    t_own, t_dp = [], None
    for h in range(2):
        wait("v", t_h[h])
        vc(src[h], bT[h][:, 0:64])
        t_sm.append(cut("v"))
        if near and rank is not None:
            vc(T.SR[:, 64 * h:64 * h + 64], bT[h][:, 0:64])
            t_own.append(cut("v"))
        if b_inv is not None and ((b_inv in lay["away"][a]) == (h == 0)):
            lb = 0 if (b_inv in lay["here"][a]) == near else 512
            vc(T.DP[:, lb + 64 * a:lb + 64 * a + 64], bT[h][:, 0:64])
            t_dp = cut("v")
    for call in calls:
        wait("g", *[t_sm[part[0]] for part in call])
        slots(call, src)
    if a_port is not None:
        own = rank is not None
        arrive("g", "n0" if own else "rf")
        slots(forward_call(lay, a_port), [T.SR[:, 0:64] if own else T.RL[:]])
    if rank is not None:
        arrive("g", "f1")
        slots(home_call(lay, cores, rank), [None, T.SR[:, 192:256]])

    if b_inv is not None:
        k = lay["own"][b_inv]
        vm(T.IW[:, DB + R // 2:DB + R], 0.0)
        t_iv = cut("v")
        wait("s", t_i3, t_late)
        op("s", S.activation(T.Ci[:], T.Ci[:], F.Identity, bias=pf(0)))
        for m in range(4):
            op("s", S.activation(T.SV[:, 128 * m:128 * m + 128], T.J128[:], F.Identity, bias=pf(14 + m), scale=pf(10)))
        for blk in range(8):
            sc(T.IW[:, DB + 512 * blk:DB + 512 * blk + 512], T.Z[:])
        t_iw = cut("s")
        arrive("p", "dl")
        wait("p", t_dp, t_late)
        for i in range(2):
            mm(T.b0[:, 0:32], T.DP[:, 512 * i + 2:512 * i + 512:4], T.Id[:, 32 * k:32 * k + 32], i == 0, False)
            mm(T.b0[:, 0:32], T.DP[:, 512 * i + 3:512 * i + 512:4], T.Ih[:, 32 * k:32 * k + 32], False, i == 1)
        wait("v", cut("p"))
        vt(T.DX[:], T.b0[:, 0:32], T.Cc[:, 0:32], A.max)
        drain("v")
        vc(T.OT[:], T.DX[:])
        drain("v")
        wait("v", t_iw, t_iv)
        vc(T.IW[:].indirect(T.OT[:]), T.SV[:])
        wait("p", cut("v"))
        tb, rb = (T.b3, T.b4), (T.b1, T.b2, T.b5, T.b6)
        t_c, t_r, t_iu = [], [], []

        def sums(n, q0=0, q1=16):
            if n >= 2:
                wait("p", t_c[n - 2])
            c0 = DB + 2048 * n
            for q in range(q0, q1):
                mm(tb[n % 2][:, q:256:16], T.IW[:, c0 + q:c0 + 2048:16], T.E1[:], True, True)
            if q1 < 16:
                return
            wait("s", cut("p"))
            sc(T.TI[:, 256 * n:256 * n + 256], tb[n % 2][:, 0:256])
            t_c.append(cut("s"))

        def turned(n):
            wait("p", t_c[n])
            c0 = 256 * n
            mm(rb[n][:, 0:128], T.TI[:, c0:c0 + 128], T.Id[:], True, False)
            mm(rb[n][:, 0:128], T.TI[:, c0 + 128:c0 + 256], T.Ih[:], False, True)
            t_r.append(cut("p"))

        sums(0)
        sums(1, 0, 8)
        turned(0)
        sums(1, 8, 16)
        sums(2, 0, 8)
        turned(1)
        sums(2, 8, 16)
        sums(3)
        turned(2)
        turned(3)
        for n in range(4):
            c0 = 128 * n
            wait("v", t_r[n])
            vt(T.IF[:, c0:c0 + 128], rb[n][:, 0:128], T.Ci[:, c0:c0 + 128], A.max)
            drain("v")
            vc(T.IV[:, c0:c0 + 128], T.IF[:, c0:c0 + 128])
            t_iu.append(cut("v"))
        if a_port is not None:
            for call in data_calls(lay, cores, a_port)[0:4]:
                if call[0] == core:
                    arrive("g", call[1])
                    blocks(a_port, call, [block(n) for n in call[2]])
        for n in range(IUP):
            wait("g", t_iu[n])
            fused([(T.IV[:, 128 * n:128 * n + 128], lay["on"][core], [(cores[b_inv], T.IU[:, 128 * n:128 * n + 128], "iu%d" % n)])],
                  T.sem.ls)

    if rank is not None:
        t_late = late_constants()
        dc = data_calls(lay, cores, rank)
        dest = [b for call in dc for b in call[4]] + [rank]
        home = lay["away"][rank] + lay["here"][rank]
        t_g = {}

        def gath(q, n, c0=0, c1=CAP):
            k = home.index(dest[n])
            o = T.comb[:, R + CAP * rank + c0:R + CAP * rank + c1] if n == 7 else T.G[:, CAP * n + c0:CAP * n + c1]
            i = T.comb[:, 0:R].indirect(T.SO[:, 32 * k + c0 // 16:32 * k + c1 // 16])
            if q == "v":
                vc(o, i)
            else:
                sc(o, i)
            t_g.setdefault(n, []).append(cut(q))

        b1, b2 = (T.b0, T.b3), (T.b1, T.b4)
        t_1, t_2, t_so = [], [], []

        def first(h):
            arrive("p", "n%d" % h)
            arrive("p", "f%d" % h)
            if t_own:
                wait("p", t_own[h])
            for i in range(2):
                c0 = 128 * i + 64 * h
                mm(b1[h][0:64, 0:128], T.SR[:, c0:c0 + 64], T.Id[:], i == 0, i == 1)
            t_1.append(cut("p"))

        def second(h):
            wait("v", t_1[h])
            vc(T.A1[0:64, 128 * h:128 * h + 128], b1[h][0:64, 0:128])
            wait("p", cut("v"), t_late)
            mm(b2[h][:, 0:128], T.Ed[0:64, :], T.A1[0:64, 128 * h:128 * h + 128], True, True)
            t_2.append(cut("p"))

        def third(h):
            wait("v", t_2[h])
            vc(T.SO[:, 128 * h:128 * h + 128], b2[h][:, 0:128])
            t_so.append(drain("v"))

        first(0)
        second(0)
        third(0)
        wait("v", t_tab)
        wait("s", t_so[0], t_tab)
        for n in range(2):
            gath("v", n, 0, CAP // 2)
            gath("s", n, CAP // 2, CAP)
        gath("s", 2)
        first(1)
        second(1)
        gath("v", 3)
        third(1)
        wait("s", t_so[1])
        gath("s", 4)
        gath("s", 6)
        gath("v", 5)
        gath("v", 7)

        if a_port is None:
            p, last_via, full = lay["port"][rank], dc[3][0], lay["full"][core]
            for n in range(2):
                wait("g", *t_g[n])
                fused([(block(n), full, [(p, block(n), "hp%d" % n)])], T.sem.ls)
            wait("g", *(t_g[2] + t_g[3]))
            m = split(full, 2)
            fused([(block(2), m[0], [(p, block(2), "hp2")]),
                   (block(3), m[1], [(last_via, block(3) if last_via == p else T.Q[:], "hq")])], T.sem.ls)
        for call in dc:
            if call[1] is None:
                wait("g", *[t for n in call[2] for t in t_g[n]])
                blocks(rank, call, [block(n) for n in call[2]])
        for x in here:
            if lay["second"][x] == core:
                arrive("g", "hq")
                blocks(x, data_calls(lay, cores, x)[3], [T.Q[:]])

        maker = lay["inv"][rank]
        for q in ("v", "s"):
            queues[q].wait_ge(T.sem.iu0, ones_of(lay["on"][maker]))
            arrive(q, "dat")
            wait(q, *t_g[7])
        c0 = 0
        for n in CH:
            for q in ("v", "s"):
                c = c0 if q == "v" else c0 + n
                if c0 and c0 * IUP % R == 0:
                    queues[q].wait_ge(T.sem["iu%d" % (c0 * IUP // R)], ones_of(lay["on"][maker]))
                i = T.comb[:].indirect(T.IU[:, c // 16:(c + n) // 16])
                if q == "v":
                    vc(T.YB[:, c:c + n], i)
                else:
                    sc(T.YB[:, c:c + n], i)
                wait("y", cut(q))
            dmas("y", [(T.y[:, c0:c0 + 2 * n], T.YB[:, c0:c0 + 2 * n])])
            c0 += 2 * n
    g.wait_ge(T.sem.ls, tot[0])
    for t in allt:
        if t[2] not in waited:
            wait("g", t)
